import numpy as np
import ml_dtypes


def mxq(x, axis, fmt="e4m3"):
    dtype, down = {"e4m3": (ml_dtypes.float8_e4m3fn, 7), "e5m2": (ml_dtypes.float8_e5m2, 14)}[fmt]
    v = np.moveaxis(np.asarray(x, np.float32).astype(ml_dtypes.bfloat16).astype(np.float64), axis, -1)
    blocks = v.reshape(v.shape[:-1] + (-1, 32))
    amax = np.abs(blocks).max(-1, keepdims=True)
    byte = np.maximum(np.where(amax > 0, np.frexp(amax)[1] - 1 + 127, 0) - down, 1)
    scale = np.exp2(byte - 127.0)
    codes = (blocks / scale).astype(np.float32).astype(dtype).astype(np.float64)
    return np.moveaxis((codes * scale).reshape(v.shape), -1, axis)


WIDE = False


def mx_kscale(k):
    if not WIDE:
        return np.ones(k)
    levels = np.array([10, -10, 5, -5, 0])
    if k % 512:
        return np.exp2(np.random.permutation(np.resize(levels, k // 32))).repeat(32)
    a = np.empty((k // 512, 16))
    for p in range(k // 512):
        a[p, :8] = np.random.permutation(np.resize(levels, 8))
        for g in range(8):
            far = levels[np.abs(levels - a[p, g]) >= 10]
            a[p, g + 8] = far[np.random.randint(len(far))]
    return np.exp2(a.ravel()).repeat(32)


def f64(x):
    return np.asarray(x).astype(np.float64)


def striped(idx):
    return np.tile(idx.reshape(-1, 16).T, (8, 1)).astype(np.uint16)


def unstriped(offs):
    return offs[:16].T.reshape(-1).astype(np.int64)


E2M1 = np.array([0.0, 0.5, 1.0, 1.5, 2.0, 3.0, 4.0, 6.0, -0.0, -0.5, -1.0, -1.5, -2.0, -3.0, -4.0, -6.0])


def pack_weight(w, fmt):
    k, n = w.shape
    w = f64(np.asarray(w, np.float32).astype(ml_dtypes.bfloat16)).reshape(k // 32, 32, n)
    amax = np.abs(w).max(1)
    if fmt == "e4m3":
        byte = np.frexp(amax)[1] - 1 + 127 - 7
    else:
        mant, ex = np.frexp(amax / 6.0)
        byte = np.where(mant > 0.5, ex, ex - 1) + 127
    byte = np.clip(np.where(amax > 0, byte, 1), 1, 254)
    scaled = (w * np.exp2(127.0 - byte)[:, None, :]).reshape(k, n).astype(np.float32)
    by_word = np.ascontiguousarray(scaled.reshape(k // 512, 128, 4, n).transpose(0, 1, 3, 2))
    if fmt == "e4m3":
        words = by_word.astype(ml_dtypes.float8_e4m3fn).view(np.uint8)
    else:
        c = by_word.astype(ml_dtypes.float4_e2m1fn).view(np.uint8) & 0xF
        words = (c[..., 0::2] | (c[..., 1::2] << 4)).reshape(k // 512, 128, 2 * n)
    return np.ascontiguousarray(words), np.ascontiguousarray(byte.astype(np.uint8).reshape(k // 512, 16, n))


def unpack_weight(words, scales, fmt):
    g, _, n = scales.shape
    words = np.ascontiguousarray(words).reshape(g, 128, n, -1)
    if fmt == "e4m3":
        vals = words.view(ml_dtypes.float8_e4m3fn).astype(np.float64)
    else:
        nib = np.empty((g, 128, n, 4), np.uint8)
        nib[..., 0::2] = words & 0xF
        nib[..., 1::2] = words >> 4
        vals = E2M1[nib]
    vals = vals * np.repeat(np.exp2(scales.astype(np.float64) - 127.0), 8, axis=1)[..., None]
    return vals.transpose(0, 1, 3, 2).reshape(g * 512, n)


def pack_table(v):
    words, scales = pack_weight(v, "e4m3")
    return np.concatenate([words.reshape(words.shape[0], -1), scales.reshape(scales.shape[0], -1)], axis=1)


def unpack_table(tab):
    g, t = tab.shape[0], tab.shape[1] // 528
    return unpack_weight(tab[:, :512 * t].reshape(g, 128, t, 4), tab[:, 512 * t:].reshape(g, 16, t), "e4m3")


def silu(v):
    return v / (1.0 + np.exp(-np.maximum(v, -700.0)))


K, M, T, S = 512, 128, 2048, 1024


def setup_inputs():
    n = np.random.standard_normal
    s = mx_kscale(K)[:, None]
    p_w4 = pack_weight(n((K, M)) / np.sqrt(K) / s, "e2m1")
    return {
        "tab": pack_table(n((K, T)) * s),
        "w4_words": p_w4[0],
        "w4_scales": p_w4[1],
        "w8": (n((K, M)) / np.sqrt(K) / s).astype(np.float32),
        "r": (n((1024, 128))).astype(np.float32),
        "offs": striped(np.random.permutation(T)[:S]),
    }


def reference(tab, w4_words, w4_scales, w8, r, offs):
    tab_ = unpack_table(tab)[:, unstriped(offs)]
    w4_ = unpack_weight(w4_words, w4_scales, "e2m1")
    w8_ = mxq(f64(w8), 0, "e4m3")
    y = tab_.T @ w4_
    u = tab_.T @ w8_
    y = silu(y) * u
    return f64(r) + y

@@ -1,0 +1,150 @@
+from contextlib import ExitStack
+
+import concourse.mybir as mybir
+
+K, M, T, S = 512, 128, 2048, 1024
+FLOPS = 2 * 2 * K * M * S
+
+P = 128
+PACK = 4
+QUADRANTS = 4
+ROWS = 4
+TABLE_WORD_BYTES = PACK * P * T
+GATHER_BLOCKS = 2
+GATHERS = S // (GATHER_BLOCKS * P)
+
+GROUPS = ((0, 2), (2, 2), (4, 2), (6, 1), (7, 1))
+
+F32 = mybir.dt.float32
+BF16 = mybir.dt.bfloat16
+I32 = mybir.dt.int32
+U32 = mybir.dt.uint32
+U16 = mybir.dt.uint16
+U8 = mybir.dt.uint8
+E4M3_X4 = mybir.dt.float8_e4m3fn_x4
+E2M1_X4 = mybir.dt.float4_e2m1fn_x4
+SILU = mybir.ActivationFunctionType.Silu
+MULT = mybir.AluOpType.mult
+ADD = mybir.AluOpType.add
+
+
+def tile_list_tabglu_tm_res_kernel(tc, tab, w4_words, w4_scales, w8, r, offs, out):
+    nc = tc.nc
+    with ExitStack() as ctx:
+        keep = ctx.enter_context(tc.tile_pool(name="keep", bufs=1))
+        psum = ctx.enter_context(tc.psum_pool(name="psum", bufs=1))
+
+        lists = keep.tile([P, S // 16], U16, name="lists")
+        tab_words = keep.tile([P, T], I32, name="tab_words", align_bytes=64)
+        tab_scales = keep.tile([P, T // 4], I32, name="tab_scales", align_bytes=64)
+        w4_codes = keep.tile([P, 2 * M], U8, name="w4_codes", align_bytes=64)
+        w4_planes = keep.tile([P, M // 4], I32, name="w4_planes", align_bytes=64)
+        w8_raw = keep.tile([P, PACK, M], F32, name="w8_raw", align_bytes=64)
+        w8_grouped = keep.tile([P, M, PACK], BF16, name="w8_grouped", tag="stage", align_bytes=64)
+        w8_codes = keep.tile([P, M], U32, name="w8_codes", align_bytes=64)
+        w8_planes = keep.tile([P, M], U8, name="w8_planes", align_bytes=64)
+        picked_words = [
+            keep.tile(
+                [P, GATHER_BLOCKS * P],
+                U32,
+                name="picked_words%d" % g,
+                tag="stage" if g == GATHERS - 1 else "picked_words%d" % g,
+                align_bytes=64,
+            )
+            for g in range(GATHERS)
+        ]
+        picked_scales = keep.tile([P, S], U8, name="picked_scales", align_bytes=64)
+        res = keep.tile([P, S // P, M], F32, name="res")
+        gates = [keep.tile([P, n, M], F32, name="gates%d" % i) for i, (b, n) in enumerate(GROUPS)]
+        prods = [keep.tile([P, n, M], F32, name="prods%d" % i) for i, (b, n) in enumerate(GROUPS)]
+        sums = [keep.tile([P, n, M], F32, name="sums%d" % i) for i, (b, n) in enumerate(GROUPS)]
+        banks = (0, 1, 2, 0, 3)
+        e_psum = [psum.tile([P, n, M], F32, name="e%d" % i, tag="e_bank%d" % banks[i]) for i, (b, n) in enumerate(GROUPS)]
+        u_psum = [psum.tile([P, n, M], F32, name="u%d" % i, tag="u_bank%d" % banks[i]) for i, (b, n) in enumerate(GROUPS)]
+        dummy = keep.tile([P, 1], F32, name="dummy")
+
+        tab_scale_rows = tab[0, TABLE_WORD_BYTES:].rearrange("(b t) -> b t", t=T).bitcast(I32)
+        w4_scale_rows = w4_scales[0].bitcast(I32)
+
+        nc.gpsimd.memset(w4_planes[:], 0)
+        nc.gpsimd.memset(dummy[:], 0.0)
+        nc.vector.memset(tab_scales[:], 0)
+        nc.vector.memset(tab_words[:, 0:8], 0)
+        nc.vector.memset(w8_raw[:, 0, 0:8], 0.0)
+
+        nc.scalar.activation(dummy[:], dummy[:], SILU)
+
+        nc.sync.dma_start(out=lists[:], in_=offs)
+        nc.sync.dma_start(out=w4_codes[:].bitcast(I32), in_=w4_words[0].bitcast(I32))
+        for q in range(QUADRANTS):
+            queue = nc.sync if q == 0 else nc.gpsimd
+            queue.dma_start(out=w4_planes[32 * q : 32 * q + ROWS, :], in_=w4_scale_rows[ROWS * q : ROWS * (q + 1), :])
+        for q in range(QUADRANTS):
+            nc.sync.dma_start(out=tab_scales[32 * q : 32 * q + ROWS, :], in_=tab_scale_rows[ROWS * q : ROWS * (q + 1), :])
+        nc.sync.dma_start(out=tab_words[:], in_=tab[0, :TABLE_WORD_BYTES].rearrange("(p t) -> p t", p=P).bitcast(I32))
+        nc.sync.dma_start(out=w8_raw[:], in_=w8.rearrange("(p j) n -> p j n", j=PACK))
+        nc.gpsimd.tensor_copy(out=res[:, 0, 0:1], in_=dummy[:])
+        nc.sync.dma_start(out=res[:], in_=r.rearrange("(b p) n -> p b n", p=P))
+
+        nc.vector.tensor_copy(out=picked_scales[:], in_=tab_scales[:].bitcast(U8).indirect(lists[:]))
+
+        nc.scalar.copy(out=w8_grouped[:], in_=w8_raw[:].rearrange("p j n -> p n j"))
+
+        def gather(g):
+            width = GATHER_BLOCKS * P // 16
+            offsets = lists[:, g * width : (g + 1) * width]
+            nc.vector.tensor_copy(out=picked_words[g][:], in_=tab_words[:].bitcast(U32).indirect(offsets))
+
+        def quantise_w8():
+            nc.vector.quantize_mx(
+                out=w8_codes[:].bitcast(E4M3_X4),
+                scales=w8_planes[:],
+                in_=w8_grouped[:].rearrange("p n j -> p (n j)"),
+            )
+
+        def multiply(bank, i, weights, weight_scales):
+            first, count = GROUPS[i]
+            for b in range(first, first + count):
+                at = b % GATHER_BLOCKS * P
+                nc.tensor.matmul_mx(
+                    out=bank[:, b - first, :],
+                    lhsT=picked_words[b // GATHER_BLOCKS][:, at : at + P].bitcast(E4M3_X4),
+                    lhsT_scale=picked_scales[:, b * P : (b + 1) * P],
+                    rhs=weights,
+                    rhs_scale=weight_scales,
+                    start=True,
+                    stop=True,
+                )
+
+        def gate(i):
+            multiply(e_psum[i], i, w4_codes[:].bitcast(E2M1_X4), w4_planes[:].bitcast(U8))
+            nc.scalar.activation(gates[i][:], e_psum[i][:], SILU)
+
+        def up(i):
+            multiply(u_psum[i], i, w8_codes[:].bitcast(E4M3_X4), w8_planes[:])
+
+        def finish(i, adder):
+            first, count = GROUPS[i]
+            nc.vector.tensor_tensor(prods[i][:], gates[i][:], u_psum[i][:], MULT)
+            adder.tensor_tensor(sums[i][:], prods[i][:], res[:, first : first + count, :], ADD)
+            rows = out[first * P : (first + count) * P, :]
+            nc.sync.dma_start(out=rows.rearrange("(b p) n -> p b n", p=P), in_=sums[i][:])
+
+        gather(0)
+        gate(0)
+        gather(1)
+        gate(1)
+        quantise_w8()
+        up(0)
+        up(1)
+        gather(2)
+        gate(2)
+        up(2)
+        finish(0, nc.gpsimd)
+        gather(3)
+        for i in (3, 4):
+            gate(i)
+            up(i)
+        finish(1, nc.gpsimd)
+        for i in (2, 3, 4):
+            finish(i, nc.vector)

@@ -38,69 +38,56 @@ def tile_list_tabglu_tm_res_kernel(tc, tab, w4_words, w4_scales, w8, r, offs, ou
         tab_words = keep.tile([P, T], I32, name="tab_words", align_bytes=64)
         tab_scales = keep.tile([P, T // 4], I32, name="tab_scales", align_bytes=64)
         w4_codes = keep.tile([P, 2 * M], U8, name="w4_codes", align_bytes=64)
-        w4_planes = keep.tile([P, M // 4], I32, name="w4_planes", align_bytes=64)
+        planes = keep.tile([P, M // 4], I32, name="planes", align_bytes=64)
         w8_raw = keep.tile([P, PACK, M], F32, name="w8_raw", align_bytes=64)
-        w8_grouped = keep.tile([P, M, PACK], BF16, name="w8_grouped", tag="stage", align_bytes=64)
+        w8_grouped = keep.tile([P, M, PACK], BF16, name="w8_grouped", align_bytes=64)
         w8_codes = keep.tile([P, M], U32, name="w8_codes", align_bytes=64)
-        w8_planes = keep.tile([P, M], U8, name="w8_planes", align_bytes=64)
         picked_words = [
-            keep.tile(
-                [P, GATHER_BLOCKS * P],
-                U32,
-                name="picked_words%d" % g,
-                tag="stage" if g == GATHERS - 1 else "picked_words%d" % g,
-                align_bytes=64,
-            )
-            for g in range(GATHERS)
+            keep.tile([P, GATHER_BLOCKS * P], U32, name="picked_words%d" % g, align_bytes=64) for g in range(GATHERS)
         ]
         picked_scales = keep.tile([P, S], U8, name="picked_scales", align_bytes=64)
         res = keep.tile([P, S // P, M], F32, name="res")
         gates = [keep.tile([P, n, M], F32, name="gates%d" % i) for i, (b, n) in enumerate(GROUPS)]
         prods = [keep.tile([P, n, M], F32, name="prods%d" % i) for i, (b, n) in enumerate(GROUPS)]
         sums = [keep.tile([P, n, M], F32, name="sums%d" % i) for i, (b, n) in enumerate(GROUPS)]
-        banks = (0, 1, 2, 0, 3)
-        e_psum = [psum.tile([P, n, M], F32, name="e%d" % i, tag="e_bank%d" % banks[i]) for i, (b, n) in enumerate(GROUPS)]
-        u_psum = [psum.tile([P, n, M], F32, name="u%d" % i, tag="u_bank%d" % banks[i]) for i, (b, n) in enumerate(GROUPS)]
+        e_banks = (0, 1, 0, 2, 1)
+        e_psum = [psum.tile([P, n, M], F32, name="e%d" % i, tag="e_bank%d" % e_banks[i]) for i, (b, n) in enumerate(GROUPS)]
+        u_psum = [psum.tile([P, n, M], F32, name="u%d" % i)[:] for i, (b, n) in enumerate(GROUPS)]
+        w4_plane = planes[:].bitcast(U8)
+        w8_plane = planes[ROWS:, :].bitcast(U8)
         dummy = keep.tile([P, 1], F32, name="dummy")
 
         tab_scale_rows = tab[0, TABLE_WORD_BYTES:].rearrange("(b t) -> b t", t=T).bitcast(I32)
         w4_scale_rows = w4_scales[0].bitcast(I32)
 
-        nc.gpsimd.memset(w4_planes[:], 0)
-        nc.gpsimd.memset(dummy[:], 0.0)
         nc.vector.memset(tab_scales[:], 0)
-        nc.vector.memset(tab_words[:, 0:8], 0)
-        nc.vector.memset(w8_raw[:, 0, 0:8], 0.0)
+        nc.gpsimd.memset(dummy[:], 0.0)
+        nc.gpsimd.memset(planes[:], 0)
 
+        nc.scalar.dma_start(out=w8_raw[:], in_=w8.rearrange("(p j) n -> p j n", j=PACK))
         nc.scalar.activation(dummy[:], dummy[:], SILU)
 
         nc.sync.dma_start(out=lists[:], in_=offs)
         nc.sync.dma_start(out=w4_codes[:].bitcast(I32), in_=w4_words[0].bitcast(I32))
         for q in range(QUADRANTS):
-            queue = nc.sync if q == 0 else nc.gpsimd
-            queue.dma_start(out=w4_planes[32 * q : 32 * q + ROWS, :], in_=w4_scale_rows[ROWS * q : ROWS * (q + 1), :])
-        for q in range(QUADRANTS):
             nc.sync.dma_start(out=tab_scales[32 * q : 32 * q + ROWS, :], in_=tab_scale_rows[ROWS * q : ROWS * (q + 1), :])
         nc.sync.dma_start(out=tab_words[:], in_=tab[0, :TABLE_WORD_BYTES].rearrange("(p t) -> p t", p=P).bitcast(I32))
-        nc.sync.dma_start(out=w8_raw[:], in_=w8.rearrange("(p j) n -> p j n", j=PACK))
-        nc.gpsimd.tensor_copy(out=res[:, 0, 0:1], in_=dummy[:])
+
+        nc.vector.tensor_copy(out=w8_grouped[:], in_=w8_raw[:].rearrange("p j n -> p n j"))
+        nc.vector.quantize_mx(
+            out=w8_codes[:].bitcast(E4M3_X4),
+            scales=w8_plane,
+            in_=w8_grouped[:].rearrange("p n j -> p (n j)"),
+        )
+        for q in range(QUADRANTS):
+            nc.sync.dma_start(out=planes[32 * q : 32 * q + ROWS, :], in_=w4_scale_rows[ROWS * q : ROWS * (q + 1), :])
         nc.sync.dma_start(out=res[:], in_=r.rearrange("(b p) n -> p b n", p=P))
-
         nc.vector.tensor_copy(out=picked_scales[:], in_=tab_scales[:].bitcast(U8).indirect(lists[:]))
-
-        nc.scalar.copy(out=w8_grouped[:], in_=w8_raw[:].rearrange("p j n -> p n j"))
 
         def gather(g):
             width = GATHER_BLOCKS * P // 16
             offsets = lists[:, g * width : (g + 1) * width]
             nc.vector.tensor_copy(out=picked_words[g][:], in_=tab_words[:].bitcast(U32).indirect(offsets))
-
-        def quantise_w8():
-            nc.vector.quantize_mx(
-                out=w8_codes[:].bitcast(E4M3_X4),
-                scales=w8_planes[:],
-                in_=w8_grouped[:].rearrange("p n j -> p (n j)"),
-            )
 
         def multiply(bank, i, weights, weight_scales):
             first, count = GROUPS[i]
@@ -117,34 +104,33 @@ def tile_list_tabglu_tm_res_kernel(tc, tab, w4_words, w4_scales, w8, r, offs, ou
                 )
 
         def gate(i):
-            multiply(e_psum[i], i, w4_codes[:].bitcast(E2M1_X4), w4_planes[:].bitcast(U8))
+            multiply(e_psum[i][:], i, w4_codes[:].bitcast(E2M1_X4), w4_plane)
             nc.scalar.activation(gates[i][:], e_psum[i][:], SILU)
 
         def up(i):
-            multiply(u_psum[i], i, w8_codes[:].bitcast(E4M3_X4), w8_planes[:])
+            multiply(u_psum[i], i, w8_codes[:].bitcast(E4M3_X4), w8_plane)
+
+        def product(i):
+            nc.vector.tensor_tensor(prods[i][:], gates[i][:], u_psum[i], MULT)
 
         def finish(i, adder):
             first, count = GROUPS[i]
-            nc.vector.tensor_tensor(prods[i][:], gates[i][:], u_psum[i][:], MULT)
             adder.tensor_tensor(sums[i][:], prods[i][:], res[:, first : first + count, :], ADD)
             rows = out[first * P : (first + count) * P, :]
             nc.sync.dma_start(out=rows.rearrange("(b p) n -> p b n", p=P), in_=sums[i][:])
 
-        gather(0)
-        gate(0)
-        gather(1)
-        gate(1)
-        quantise_w8()
-        up(0)
-        up(1)
-        gather(2)
-        gate(2)
-        up(2)
-        finish(0, nc.gpsimd)
-        gather(3)
-        for i in (3, 4):
+        for g in range(GATHERS):
+            gather(g)
+        for i in range(len(GROUPS)):
             gate(i)
             up(i)
-        finish(1, nc.gpsimd)
-        for i in (2, 3, 4):
-            finish(i, nc.vector)
+        product(0)
+        finish(0, nc.gpsimd)
+        product(1)
+        product(2)
+        finish(1, nc.vector)
+        finish(2, nc.gpsimd)
+        product(3)
+        product(4)
+        finish(3, nc.vector)
+        finish(4, nc.vector)

@@ -69,8 +69,8 @@ def tile_list_tabglu_tm_res_kernel(tc, tab, w4_words, w4_scales, w8, r, offs, ou
 
         nc.sync.dma_start(out=lists[:], in_=offs)
         nc.sync.dma_start(out=w4_codes[:].bitcast(I32), in_=w4_words[0].bitcast(I32))
-        for q in range(QUADRANTS):
-            nc.sync.dma_start(out=tab_scales[32 * q : 32 * q + ROWS, :], in_=tab_scale_rows[ROWS * q : ROWS * (q + 1), :])
+        for i in range(ROWS):
+            nc.sync.dma_start(out=tab_scales[i:P:32, :], in_=tab_scale_rows[i : ROWS * QUADRANTS : ROWS, :])
         nc.sync.dma_start(out=tab_words[:], in_=tab[0, :TABLE_WORD_BYTES].rearrange("(p t) -> p t", p=P).bitcast(I32))
 
         nc.vector.tensor_copy(out=w8_grouped[:], in_=w8_raw[:].rearrange("p j n -> p n j"))
@@ -121,9 +121,13 @@ def tile_list_tabglu_tm_res_kernel(tc, tab, w4_words, w4_scales, w8, r, offs, ou
 
         for g in range(GATHERS):
             gather(g)
-        for i in range(len(GROUPS)):
+        for i in range(3):
             gate(i)
             up(i)
+        gate(3)
+        gate(4)
+        up(3)
+        up(4)
         product(0)
         finish(0, nc.gpsimd)
         product(1)

@@ -55,6 +55,7 @@ def tile_list_tabglu_tm_res_kernel(tc, tab, w4_words, w4_scales, w8, r, offs, ou
         u_psum = [psum.tile([P, n, M], F32, name="u%d" % i)[:] for i, (b, n) in enumerate(GROUPS)]
         w4_plane = planes[:].bitcast(U8)
         w8_plane = planes[ROWS:, :].bitcast(U8)
+        u_first = keep.tile([P, GROUPS[0][1], M], F32, name="u_first")
         dummy = keep.tile([P, 1], F32, name="dummy")
 
         tab_scale_rows = tab[0, TABLE_WORD_BYTES:].rearrange("(b t) -> b t", t=T).bitcast(I32)
@@ -109,9 +110,14 @@ def tile_list_tabglu_tm_res_kernel(tc, tab, w4_words, w4_scales, w8, r, offs, ou
 
         def up(i):
             multiply(u_psum[i], i, w8_codes[:].bitcast(E4M3_X4), w8_plane)
+            if i == 0:
+                nc.scalar.copy(out=u_first[:], in_=u_psum[i])
 
         def product(i):
-            nc.vector.tensor_tensor(prods[i][:], gates[i][:], u_psum[i], MULT)
+            if i == 0:
+                nc.gpsimd.tensor_tensor(prods[i][:], gates[i][:], u_first[:], MULT)
+            else:
+                nc.vector.tensor_tensor(prods[i][:], gates[i][:], u_psum[i], MULT)
 
         def finish(i, adder):
             first, count = GROUPS[i]
@@ -133,7 +139,7 @@ def tile_list_tabglu_tm_res_kernel(tc, tab, w4_words, w4_scales, w8, r, offs, ou
         product(1)
         product(2)
         finish(1, nc.vector)
-        finish(2, nc.gpsimd)
+        finish(2, nc.vector)
         product(3)
         product(4)
         finish(3, nc.vector)

@@ -11,9 +11,10 @@ QUADRANTS = 4
 ROWS = 4
 TABLE_WORD_BYTES = PACK * P * T
 GATHER_BLOCKS = 2
+EARLY = 768
 GATHERS = S // (GATHER_BLOCKS * P)
 
-GROUPS = ((0, 2), (2, 2), (4, 2), (6, 1), (7, 1))
+GROUPS = ((0, 1), (1, 1), (2, 2), (4, 2), (6, 1), (7, 1))
 
 F32 = mybir.dt.float32
 BF16 = mybir.dt.bfloat16
@@ -45,17 +46,19 @@ def tile_list_tabglu_tm_res_kernel(tc, tab, w4_words, w4_scales, w8, r, offs, ou
         picked_words = [
             keep.tile([P, GATHER_BLOCKS * P], U32, name="picked_words%d" % g, align_bytes=64) for g in range(GATHERS)
         ]
-        picked_scales = keep.tile([P, S], U8, name="picked_scales", align_bytes=64)
+        picked_scales = keep.tile([P, EARLY], U8, name="picked_scales", align_bytes=64)
+        late_scales = keep.tile([P, S - EARLY], U8, name="late_scales", tag="picked_words0", align_bytes=64)
         res = keep.tile([P, S // P, M], F32, name="res")
         gates = [keep.tile([P, n, M], F32, name="gates%d" % i) for i, (b, n) in enumerate(GROUPS)]
         prods = [keep.tile([P, n, M], F32, name="prods%d" % i) for i, (b, n) in enumerate(GROUPS)]
         sums = [keep.tile([P, n, M], F32, name="sums%d" % i) for i, (b, n) in enumerate(GROUPS)]
-        e_banks = (0, 1, 0, 2, 1)
+        e_banks = (0, 1, 2, 0, 1, 3)
+        u_banks = (0, 1, 2, 0, 1, 3)
         e_psum = [psum.tile([P, n, M], F32, name="e%d" % i, tag="e_bank%d" % e_banks[i]) for i, (b, n) in enumerate(GROUPS)]
-        u_psum = [psum.tile([P, n, M], F32, name="u%d" % i)[:] for i, (b, n) in enumerate(GROUPS)]
+        u_psum = [psum.tile([P, n, M], F32, name="u%d" % i, tag="u_bank%d" % u_banks[i])[:] for i, (b, n) in enumerate(GROUPS)]
         w4_plane = planes[:].bitcast(U8)
         w8_plane = planes[ROWS:, :].bitcast(U8)
-        u_first = keep.tile([P, GROUPS[0][1], M], F32, name="u_first")
+        u_first = [keep.tile([P, 1, M], F32, name="u_first%d" % i) for i in range(2)]
         dummy = keep.tile([P, 1], F32, name="dummy")
 
         tab_scale_rows = tab[0, TABLE_WORD_BYTES:].rearrange("(b t) -> b t", t=T).bitcast(I32)
@@ -83,7 +86,7 @@ def tile_list_tabglu_tm_res_kernel(tc, tab, w4_words, w4_scales, w8, r, offs, ou
         for q in range(QUADRANTS):
             nc.sync.dma_start(out=planes[32 * q : 32 * q + ROWS, :], in_=w4_scale_rows[ROWS * q : ROWS * (q + 1), :])
         nc.sync.dma_start(out=res[:], in_=r.rearrange("(b p) n -> p b n", p=P))
-        nc.vector.tensor_copy(out=picked_scales[:], in_=tab_scales[:].bitcast(U8).indirect(lists[:]))
+        nc.vector.tensor_copy(out=picked_scales[:], in_=tab_scales[:].bitcast(U8).indirect(lists[:, : EARLY // 16]))
 
         def gather(g):
             width = GATHER_BLOCKS * P // 16
@@ -97,7 +100,7 @@ def tile_list_tabglu_tm_res_kernel(tc, tab, w4_words, w4_scales, w8, r, offs, ou
                 nc.tensor.matmul_mx(
                     out=bank[:, b - first, :],
                     lhsT=picked_words[b // GATHER_BLOCKS][:, at : at + P].bitcast(E4M3_X4),
-                    lhsT_scale=picked_scales[:, b * P : (b + 1) * P],
+                    lhsT_scale=picked_scales[:, b * P : (b + 1) * P] if b * P < EARLY else late_scales[:, at : at + P],
                     rhs=weights,
                     rhs_scale=weight_scales,
                     start=True,
@@ -110,12 +113,12 @@ def tile_list_tabglu_tm_res_kernel(tc, tab, w4_words, w4_scales, w8, r, offs, ou
 
         def up(i):
             multiply(u_psum[i], i, w8_codes[:].bitcast(E4M3_X4), w8_plane)
-            if i == 0:
-                nc.scalar.copy(out=u_first[:], in_=u_psum[i])
+            if i < 2:
+                nc.scalar.copy(out=u_first[i][:], in_=u_psum[i])
 
         def product(i):
-            if i == 0:
-                nc.gpsimd.tensor_tensor(prods[i][:], gates[i][:], u_first[:], MULT)
+            if i < 2:
+                nc.gpsimd.tensor_tensor(prods[i][:], gates[i][:], u_first[i][:], MULT)
             else:
                 nc.vector.tensor_tensor(prods[i][:], gates[i][:], u_psum[i], MULT)
 
@@ -127,20 +130,22 @@ def tile_list_tabglu_tm_res_kernel(tc, tab, w4_words, w4_scales, w8, r, offs, ou
 
         for g in range(GATHERS):
             gather(g)
-        for i in range(3):
+        for i in range(4):
             gate(i)
             up(i)
-        gate(3)
+        nc.vector.tensor_copy(out=late_scales[:], in_=tab_scales[:].bitcast(U8).indirect(lists[:, EARLY // 16 :]))
         gate(4)
-        up(3)
+        gate(5)
         up(4)
-        product(0)
-        finish(0, nc.gpsimd)
-        product(1)
+        up(5)
+        for i in (0, 1):
+            product(i)
+            finish(i, nc.gpsimd)
         product(2)
-        finish(1, nc.vector)
-        finish(2, nc.vector)
         product(3)
-        product(4)
+        finish(2, nc.vector)
         finish(3, nc.vector)
+        product(4)
+        product(5)
         finish(4, nc.vector)
+        finish(5, nc.vector)

@@ -12,6 +12,8 @@ ROWS = 4
 TABLE_WORD_BYTES = PACK * P * T
 GATHER_BLOCKS = 2
 EARLY = 768
+HEAD = 256
+SHARE = 48
 GATHERS = S // (GATHER_BLOCKS * P)
 
 GROUPS = ((0, 1), (1, 1), (2, 2), (4, 2), (6, 1), (7, 1))
@@ -68,16 +70,19 @@ def tile_list_tabglu_tm_res_kernel(tc, tab, w4_words, w4_scales, w8, r, offs, ou
         nc.gpsimd.memset(dummy[:], 0.0)
         nc.gpsimd.memset(planes[:], 0)
 
-        nc.scalar.dma_start(out=w8_raw[:], in_=w8.rearrange("(p j) n -> p j n", j=PACK))
+        nc.sync.dma_start(out=w8_raw[:], in_=w8.rearrange("(p j) n -> p j n", j=PACK))
         nc.scalar.activation(dummy[:], dummy[:], SILU)
 
         nc.sync.dma_start(out=lists[:], in_=offs)
-        nc.sync.dma_start(out=w4_codes[:].bitcast(I32), in_=w4_words[0].bitcast(I32))
+        word_rows = tab[0, :TABLE_WORD_BYTES].rearrange("(p t) -> p t", p=P).bitcast(I32)
+        nc.sync.dma_start(out=tab_words[:, :HEAD], in_=word_rows[:, :HEAD])
         for i in range(ROWS):
             nc.sync.dma_start(out=tab_scales[i:P:32, :], in_=tab_scale_rows[i : ROWS * QUADRANTS : ROWS, :])
-        nc.sync.dma_start(out=tab_words[:], in_=tab[0, :TABLE_WORD_BYTES].rearrange("(p t) -> p t", p=P).bitcast(I32))
+        nc.sync.dma_start(out=tab_words[:, HEAD:], in_=word_rows[:, HEAD:])
+        nc.sync.dma_start(out=w4_codes[:].bitcast(I32), in_=w4_words[0].bitcast(I32))
 
-        nc.vector.tensor_copy(out=w8_grouped[:], in_=w8_raw[:].rearrange("p j n -> p n j"))
+        nc.scalar.copy(out=w8_grouped[:, :SHARE, :], in_=w8_raw[:, :, :SHARE].rearrange("p j n -> p n j"))
+        nc.vector.tensor_copy(out=w8_grouped[:, SHARE:, :], in_=w8_raw[:, :, SHARE:].rearrange("p j n -> p n j"))
         nc.vector.quantize_mx(
             out=w8_codes[:].bitcast(E4M3_X4),
             scales=w8_plane,
@@ -138,11 +143,12 @@ def tile_list_tabglu_tm_res_kernel(tc, tab, w4_words, w4_scales, w8, r, offs, ou
         gate(5)
         up(4)
         up(5)
-        for i in (0, 1):
-            product(i)
-            finish(i, nc.gpsimd)
+        product(0)
+        finish(0, nc.gpsimd)
+        product(1)
         product(2)
         product(3)
+        finish(1, nc.vector)
         finish(2, nc.vector)
         finish(3, nc.vector)
         product(4)

@@ -68,7 +68,6 @@ def tile_list_tabglu_tm_res_kernel(tc, tab, w4_words, w4_scales, w8, r, offs, ou
 
         nc.vector.memset(tab_scales[:], 0)
         nc.gpsimd.memset(dummy[:], 0.0)
-        nc.gpsimd.memset(planes[:], 0)
 
         nc.sync.dma_start(out=w8_raw[:], in_=w8.rearrange("(p j) n -> p j n", j=PACK))
         nc.scalar.activation(dummy[:], dummy[:], SILU)
@@ -81,8 +80,11 @@ def tile_list_tabglu_tm_res_kernel(tc, tab, w4_words, w4_scales, w8, r, offs, ou
         nc.sync.dma_start(out=tab_words[:, HEAD:], in_=word_rows[:, HEAD:])
         nc.sync.dma_start(out=w4_codes[:].bitcast(I32), in_=w4_words[0].bitcast(I32))
 
-        nc.scalar.copy(out=w8_grouped[:, :SHARE, :], in_=w8_raw[:, :, :SHARE].rearrange("p j n -> p n j"))
-        nc.vector.tensor_copy(out=w8_grouped[:, SHARE:, :], in_=w8_raw[:, :, SHARE:].rearrange("p j n -> p n j"))
+        for copy, cols in ((nc.scalar.copy, slice(0, SHARE)), (nc.vector.tensor_copy, slice(SHARE, M))):
+            copy(
+                out=w8_grouped[:, cols, :].rearrange("p (c i) j -> p c j i", i=4),
+                in_=w8_raw[:, :, cols].rearrange("p j (c i) -> p c j i", i=4),
+            )
         nc.vector.quantize_mx(
             out=w8_codes[:].bitcast(E4M3_X4),
             scales=w8_plane,

@@ -13,7 +13,6 @@ TABLE_WORD_BYTES = PACK * P * T
 GATHER_BLOCKS = 2
 EARLY = 768
 HEAD = 256
-SHARE = 48
 GATHERS = S // (GATHER_BLOCKS * P)
 
 GROUPS = ((0, 1), (1, 1), (2, 2), (4, 2), (6, 1), (7, 1))
@@ -80,11 +79,10 @@ def tile_list_tabglu_tm_res_kernel(tc, tab, w4_words, w4_scales, w8, r, offs, ou
         nc.sync.dma_start(out=tab_words[:, HEAD:], in_=word_rows[:, HEAD:])
         nc.sync.dma_start(out=w4_codes[:].bitcast(I32), in_=w4_words[0].bitcast(I32))
 
-        for copy, cols in ((nc.scalar.copy, slice(0, SHARE)), (nc.vector.tensor_copy, slice(SHARE, M))):
-            copy(
-                out=w8_grouped[:, cols, :].rearrange("p (c i) j -> p c j i", i=4),
-                in_=w8_raw[:, :, cols].rearrange("p j (c i) -> p c j i", i=4),
-            )
+        nc.vector.tensor_copy(
+            out=w8_grouped[:].rearrange("p (c i) j -> p c j i", i=4),
+            in_=w8_raw[:].rearrange("p j (c i) -> p c j i", i=4),
+        )
         nc.vector.quantize_mx(
             out=w8_codes[:].bitcast(E4M3_X4),
             scales=w8_plane,

@@ -11,8 +11,8 @@ QUADRANTS = 4
 ROWS = 4
 TABLE_WORD_BYTES = PACK * P * T
 GATHER_BLOCKS = 2
-EARLY = 768
-HEAD = 256
+HALF = S // 2
+STAGED = P - ROWS * QUADRANTS
 GATHERS = S // (GATHER_BLOCKS * P)
 
 GROUPS = ((0, 1), (1, 1), (2, 2), (4, 2), (6, 1), (7, 1))
@@ -34,6 +34,7 @@ def tile_list_tabglu_tm_res_kernel(tc, tab, w4_words, w4_scales, w8, r, offs, ou
     nc = tc.nc
     with ExitStack() as ctx:
         keep = ctx.enter_context(tc.tile_pool(name="keep", bufs=1))
+        reuse = ctx.enter_context(tc.tile_pool(name="reuse", bufs=1))
         psum = ctx.enter_context(tc.psum_pool(name="psum", bufs=1))
 
         lists = keep.tile([P, S // 16], U16, name="lists")
@@ -41,57 +42,73 @@ def tile_list_tabglu_tm_res_kernel(tc, tab, w4_words, w4_scales, w8, r, offs, ou
         tab_scales = keep.tile([P, T // 4], I32, name="tab_scales", align_bytes=64)
         w4_codes = keep.tile([P, 2 * M], U8, name="w4_codes", align_bytes=64)
         planes = keep.tile([P, M // 4], I32, name="planes", align_bytes=64)
-        w8_raw = keep.tile([P, PACK, M], F32, name="w8_raw", align_bytes=64)
-        w8_grouped = keep.tile([P, M, PACK], BF16, name="w8_grouped", align_bytes=64)
+        w8_raw = reuse.tile([P, PACK, M], F32, name="w8_raw", align_bytes=64, offset=0)
+        w8_grouped = reuse.tile([P, M, PACK], BF16, name="w8_grouped", align_bytes=64, offset=3072)
         w8_codes = keep.tile([P, M], U32, name="w8_codes", align_bytes=64)
         picked_words = [
             keep.tile([P, GATHER_BLOCKS * P], U32, name="picked_words%d" % g, align_bytes=64) for g in range(GATHERS)
         ]
-        picked_scales = keep.tile([P, EARLY], U8, name="picked_scales", align_bytes=64)
-        late_scales = keep.tile([P, S - EARLY], U8, name="late_scales", tag="picked_words0", align_bytes=64)
-        res = keep.tile([P, S // P, M], F32, name="res")
+        picked_scales = [
+            keep.tile([P, HALF], U8, name="picked_scales0", align_bytes=64),
+            reuse.tile([P, HALF], U8, name="picked_scales1", align_bytes=64, offset=0),
+        ]
+        token_planes = [keep.tile([P, HALF // 4], I32, name="token_planes%d" % h, align_bytes=64) for h in range(2)]
+        res = [
+            reuse.tile([P, HALF // P, M], F32, name="res%d" % h, align_bytes=64, offset=at)
+            for h, at in enumerate((1024, 3072))
+        ]
         gates = [keep.tile([P, n, M], F32, name="gates%d" % i) for i, (b, n) in enumerate(GROUPS)]
         prods = [keep.tile([P, n, M], F32, name="prods%d" % i) for i, (b, n) in enumerate(GROUPS)]
-        sums = [keep.tile([P, n, M], F32, name="sums%d" % i) for i, (b, n) in enumerate(GROUPS)]
+        sums = [
+            keep.tile([P, n, M], F32, name="sums%d" % i, tag="picked_words2" if i == 2 else "sums%d" % i, align_bytes=64)
+            for i, (b, n) in enumerate(GROUPS)
+        ]
         e_banks = (0, 1, 2, 0, 1, 3)
         u_banks = (0, 1, 2, 0, 1, 3)
         e_psum = [psum.tile([P, n, M], F32, name="e%d" % i, tag="e_bank%d" % e_banks[i]) for i, (b, n) in enumerate(GROUPS)]
         u_psum = [psum.tile([P, n, M], F32, name="u%d" % i, tag="u_bank%d" % u_banks[i])[:] for i, (b, n) in enumerate(GROUPS)]
         w4_plane = planes[:].bitcast(U8)
         w8_plane = planes[ROWS:, :].bitcast(U8)
-        u_first = [keep.tile([P, 1, M], F32, name="u_first%d" % i) for i in range(2)]
         dummy = keep.tile([P, 1], F32, name="dummy")
 
         tab_scale_rows = tab[0, TABLE_WORD_BYTES:].rearrange("(b t) -> b t", t=T).bitcast(I32)
         w4_scale_rows = w4_scales[0].bitcast(I32)
 
-        nc.vector.memset(tab_scales[:], 0)
+        nc.vector.memset(tab_scales[:STAGED, :], 0)
+        for h in range(2):
+            nc.vector.memset(token_planes[h][:], 0)
         nc.gpsimd.memset(dummy[:], 0.0)
 
+        nc.sync.dma_start(out=tab_scales[STAGED:, :], in_=tab_scale_rows)
+        nc.sync.dma_start(out=lists[:], in_=offs)
         nc.sync.dma_start(out=w8_raw[:], in_=w8.rearrange("(p j) n -> p j n", j=PACK))
+        word_rows = tab[0, :TABLE_WORD_BYTES].rearrange("(p t) -> p t", p=P).bitcast(I32)
+        for q in range(1, QUADRANTS):
+            nc.sync.dma_start(out=planes[32 * q : 32 * q + ROWS, :], in_=w4_scale_rows[ROWS * q : ROWS * (q + 1), :])
+        nc.sync.dma_start(out=tab_words[:], in_=word_rows)
+        nc.sync.dma_start(out=planes[:ROWS, :], in_=w4_scale_rows[:ROWS, :])
+        nc.sync.dma_start(out=w4_codes[:].bitcast(I32), in_=w4_words[0].bitcast(I32))
         nc.scalar.activation(dummy[:], dummy[:], SILU)
 
-        nc.sync.dma_start(out=lists[:], in_=offs)
-        word_rows = tab[0, :TABLE_WORD_BYTES].rearrange("(p t) -> p t", p=P).bitcast(I32)
-        nc.sync.dma_start(out=tab_words[:, :HEAD], in_=word_rows[:, :HEAD])
-        for i in range(ROWS):
-            nc.sync.dma_start(out=tab_scales[i:P:32, :], in_=tab_scale_rows[i : ROWS * QUADRANTS : ROWS, :])
-        nc.sync.dma_start(out=tab_words[:, HEAD:], in_=word_rows[:, HEAD:])
-        nc.sync.dma_start(out=w4_codes[:].bitcast(I32), in_=w4_words[0].bitcast(I32))
-
-        nc.vector.tensor_copy(
+        nc.scalar.copy(
             out=w8_grouped[:].rearrange("p (c i) j -> p c j i", i=4),
             in_=w8_raw[:].rearrange("p j (c i) -> p c j i", i=4),
         )
+        for h in range(2):
+            offsets = lists[:, h * HALF // 16 : (h + 1) * HALF // 16]
+            nc.vector.tensor_copy(out=picked_scales[h][:], in_=tab_scales[:].bitcast(U8).indirect(offsets))
         nc.vector.quantize_mx(
             out=w8_codes[:].bitcast(E4M3_X4),
             scales=w8_plane,
             in_=w8_grouped[:].rearrange("p n j -> p (n j)"),
         )
-        for q in range(QUADRANTS):
-            nc.sync.dma_start(out=planes[32 * q : 32 * q + ROWS, :], in_=w4_scale_rows[ROWS * q : ROWS * (q + 1), :])
-        nc.sync.dma_start(out=res[:], in_=r.rearrange("(b p) n -> p b n", p=P))
-        nc.vector.tensor_copy(out=picked_scales[:], in_=tab_scales[:].bitcast(U8).indirect(lists[:, : EARLY // 16]))
+        for h in range(2):
+            for q in range(QUADRANTS):
+                nc.sync.dma_start(
+                    out=token_planes[h][32 * q : 32 * q + ROWS, :],
+                    in_=picked_scales[h][:].bitcast(I32)[STAGED + ROWS * q : STAGED + ROWS * (q + 1), :],
+                )
+            nc.sync.dma_start(out=res[h][:], in_=r[h * HALF : (h + 1) * HALF, :].rearrange("(b p) n -> p b n", p=P))
 
         def gather(g):
             width = GATHER_BLOCKS * P // 16
@@ -105,7 +122,7 @@ def tile_list_tabglu_tm_res_kernel(tc, tab, w4_words, w4_scales, w8, r, offs, ou
                 nc.tensor.matmul_mx(
                     out=bank[:, b - first, :],
                     lhsT=picked_words[b // GATHER_BLOCKS][:, at : at + P].bitcast(E4M3_X4),
-                    lhsT_scale=picked_scales[:, b * P : (b + 1) * P] if b * P < EARLY else late_scales[:, at : at + P],
+                    lhsT_scale=token_planes[b * P // HALF][:].bitcast(U8)[:, b * P % HALF : b * P % HALF + P],
                     rhs=weights,
                     rhs_scale=weight_scales,
                     start=True,
@@ -118,18 +135,13 @@ def tile_list_tabglu_tm_res_kernel(tc, tab, w4_words, w4_scales, w8, r, offs, ou
 
         def up(i):
             multiply(u_psum[i], i, w8_codes[:].bitcast(E4M3_X4), w8_plane)
-            if i < 2:
-                nc.scalar.copy(out=u_first[i][:], in_=u_psum[i])
 
         def product(i):
-            if i < 2:
-                nc.gpsimd.tensor_tensor(prods[i][:], gates[i][:], u_first[i][:], MULT)
-            else:
-                nc.vector.tensor_tensor(prods[i][:], gates[i][:], u_psum[i], MULT)
+            nc.vector.tensor_tensor(prods[i][:], gates[i][:], u_psum[i], MULT)
 
         def finish(i, adder):
             first, count = GROUPS[i]
-            adder.tensor_tensor(sums[i][:], prods[i][:], res[:, first : first + count, :], ADD)
+            adder.tensor_tensor(sums[i][:], prods[i][:], res[first * P // HALF][:, first % 4 : first % 4 + count, :], ADD)
             rows = out[first * P : (first + count) * P, :]
             nc.sync.dma_start(out=rows.rearrange("(b p) n -> p b n", p=P), in_=sums[i][:])
 
@@ -138,20 +150,19 @@ def tile_list_tabglu_tm_res_kernel(tc, tab, w4_words, w4_scales, w8, r, offs, ou
         for i in range(4):
             gate(i)
             up(i)
-        nc.vector.tensor_copy(out=late_scales[:], in_=tab_scales[:].bitcast(U8).indirect(lists[:, EARLY // 16 :]))
         gate(4)
         gate(5)
         up(4)
         up(5)
         product(0)
-        finish(0, nc.gpsimd)
         product(1)
+        finish(0, nc.gpsimd)
+        finish(1, nc.gpsimd)
         product(2)
         product(3)
-        finish(1, nc.vector)
         finish(2, nc.vector)
-        finish(3, nc.vector)
         product(4)
         product(5)
+        finish(3, nc.vector)
         finish(4, nc.vector)
         finish(5, nc.vector)

@@ -15,7 +15,7 @@ HALF = S // 2
 STAGED = P - ROWS * QUADRANTS
 GATHERS = S // (GATHER_BLOCKS * P)
 
-GROUPS = ((0, 1), (1, 1), (2, 2), (4, 2), (6, 1), (7, 1))
+GROUPS = ((0, 2), (2, 2), (4, 2), (6, 1), (7, 1))
 
 F32 = mybir.dt.float32
 BF16 = mybir.dt.bfloat16
@@ -48,10 +48,7 @@ def tile_list_tabglu_tm_res_kernel(tc, tab, w4_words, w4_scales, w8, r, offs, ou
         picked_words = [
             keep.tile([P, GATHER_BLOCKS * P], U32, name="picked_words%d" % g, align_bytes=64) for g in range(GATHERS)
         ]
-        picked_scales = [
-            keep.tile([P, HALF], U8, name="picked_scales0", align_bytes=64),
-            reuse.tile([P, HALF], U8, name="picked_scales1", align_bytes=64, offset=0),
-        ]
+        picked_scales = [keep.tile([P, HALF], U8, name="picked_scales%d" % h, align_bytes=64) for h in range(2)]
         token_planes = [keep.tile([P, HALF // 4], I32, name="token_planes%d" % h, align_bytes=64) for h in range(2)]
         res = [
             reuse.tile([P, HALF // P, M], F32, name="res%d" % h, align_bytes=64, offset=at)
@@ -59,12 +56,9 @@ def tile_list_tabglu_tm_res_kernel(tc, tab, w4_words, w4_scales, w8, r, offs, ou
         ]
         gates = [keep.tile([P, n, M], F32, name="gates%d" % i) for i, (b, n) in enumerate(GROUPS)]
         prods = [keep.tile([P, n, M], F32, name="prods%d" % i) for i, (b, n) in enumerate(GROUPS)]
-        sums = [
-            keep.tile([P, n, M], F32, name="sums%d" % i, tag="picked_words2" if i == 2 else "sums%d" % i, align_bytes=64)
-            for i, (b, n) in enumerate(GROUPS)
-        ]
-        e_banks = (0, 1, 2, 0, 1, 3)
-        u_banks = (0, 1, 2, 0, 1, 3)
+        sums = [keep.tile([P, n, M], F32, name="sums%d" % i) for i, (b, n) in enumerate(GROUPS)]
+        e_banks = (0, 1, 2, 0, 1)
+        u_banks = (0, 1, 2, 3, 4)
         e_psum = [psum.tile([P, n, M], F32, name="e%d" % i, tag="e_bank%d" % e_banks[i]) for i, (b, n) in enumerate(GROUPS)]
         u_psum = [psum.tile([P, n, M], F32, name="u%d" % i, tag="u_bank%d" % u_banks[i])[:] for i, (b, n) in enumerate(GROUPS)]
         w4_plane = planes[:].bitcast(U8)
@@ -147,22 +141,20 @@ def tile_list_tabglu_tm_res_kernel(tc, tab, w4_words, w4_scales, w8, r, offs, ou
 
         for g in range(GATHERS):
             gather(g)
-        for i in range(4):
+        for i in range(3):
             gate(i)
             up(i)
+        gate(3)
         gate(4)
-        gate(5)
+        up(3)
         up(4)
-        up(5)
         product(0)
         product(1)
-        finish(0, nc.gpsimd)
+        finish(0, nc.vector)
         finish(1, nc.gpsimd)
         product(2)
         product(3)
-        finish(2, nc.vector)
         product(4)
-        product(5)
+        finish(2, nc.vector)
         finish(3, nc.vector)
         finish(4, nc.vector)
-        finish(5, nc.vector)

@@ -63,7 +63,6 @@ def tile_list_tabglu_tm_res_kernel(tc, tab, w4_words, w4_scales, w8, r, offs, ou
         u_psum = [psum.tile([P, n, M], F32, name="u%d" % i, tag="u_bank%d" % u_banks[i])[:] for i, (b, n) in enumerate(GROUPS)]
         w4_plane = planes[:].bitcast(U8)
         w8_plane = planes[ROWS:, :].bitcast(U8)
-        dummy = keep.tile([P, 1], F32, name="dummy")
 
         tab_scale_rows = tab[0, TABLE_WORD_BYTES:].rearrange("(b t) -> b t", t=T).bitcast(I32)
         w4_scale_rows = w4_scales[0].bitcast(I32)
@@ -71,7 +70,6 @@ def tile_list_tabglu_tm_res_kernel(tc, tab, w4_words, w4_scales, w8, r, offs, ou
         nc.vector.memset(tab_scales[:STAGED, :], 0)
         for h in range(2):
             nc.vector.memset(token_planes[h][:], 0)
-        nc.gpsimd.memset(dummy[:], 0.0)
 
         nc.sync.dma_start(out=tab_scales[STAGED:, :], in_=tab_scale_rows)
         nc.sync.dma_start(out=lists[:], in_=offs)
@@ -82,7 +80,6 @@ def tile_list_tabglu_tm_res_kernel(tc, tab, w4_words, w4_scales, w8, r, offs, ou
         nc.sync.dma_start(out=tab_words[:], in_=word_rows)
         nc.sync.dma_start(out=planes[:ROWS, :], in_=w4_scale_rows[:ROWS, :])
         nc.sync.dma_start(out=w4_codes[:].bitcast(I32), in_=w4_words[0].bitcast(I32))
-        nc.scalar.activation(dummy[:], dummy[:], SILU)
 
         nc.scalar.copy(
             out=w8_grouped[:].rearrange("p (c i) j -> p c j i", i=4),

@@ -14,8 +14,9 @@ GATHER_BLOCKS = 2
 HALF = S // 2
 STAGED = P - ROWS * QUADRANTS
 GATHERS = S // (GATHER_BLOCKS * P)
+HEAD = 768
 
-GROUPS = ((0, 2), (2, 2), (4, 2), (6, 1), (7, 1))
+GROUPS = ((0, 2), (2, 2), (4, 2), (6, 2))
 
 F32 = mybir.dt.float32
 BF16 = mybir.dt.bfloat16
@@ -41,65 +42,65 @@ def tile_list_tabglu_tm_res_kernel(tc, tab, w4_words, w4_scales, w8, r, offs, ou
         tab_words = keep.tile([P, T], I32, name="tab_words", align_bytes=64)
         tab_scales = keep.tile([P, T // 4], I32, name="tab_scales", align_bytes=64)
         w4_codes = keep.tile([P, 2 * M], U8, name="w4_codes", align_bytes=64)
-        planes = keep.tile([P, M // 4], I32, name="planes", align_bytes=64)
+        w4_planes = keep.tile([P, M // 4], I32, name="w4_planes", align_bytes=64)
+        w8_planes = keep.tile([P, M], U8, name="w8_planes", align_bytes=64)
         w8_raw = reuse.tile([P, PACK, M], F32, name="w8_raw", align_bytes=64, offset=0)
-        w8_grouped = reuse.tile([P, M, PACK], BF16, name="w8_grouped", align_bytes=64, offset=3072)
+        w8_grouped = keep.tile([P, M, PACK], BF16, name="w8_grouped", align_bytes=64)
         w8_codes = keep.tile([P, M], U32, name="w8_codes", align_bytes=64)
         picked_words = [
-            keep.tile([P, GATHER_BLOCKS * P], U32, name="picked_words%d" % g, align_bytes=64) for g in range(GATHERS)
+            keep.tile([P, GATHER_BLOCKS * P], U32, name="picked_words%d" % g, align_bytes=64)
+            for g in range(GATHERS - 1)
         ]
+        picked_words.append(reuse.tile([P, GATHER_BLOCKS * P], U32, name="picked_last", align_bytes=64, offset=0))
         picked_scales = [keep.tile([P, HALF], U8, name="picked_scales%d" % h, align_bytes=64) for h in range(2)]
         token_planes = [keep.tile([P, HALF // 4], I32, name="token_planes%d" % h, align_bytes=64) for h in range(2)]
-        res = [
-            reuse.tile([P, HALF // P, M], F32, name="res%d" % h, align_bytes=64, offset=at)
-            for h, at in enumerate((1024, 3072))
-        ]
+        res = [keep.tile([P, HALF // P, M], F32, name="res%d" % h, align_bytes=64) for h in range(2)]
         gates = [keep.tile([P, n, M], F32, name="gates%d" % i) for i, (b, n) in enumerate(GROUPS)]
         prods = [keep.tile([P, n, M], F32, name="prods%d" % i) for i, (b, n) in enumerate(GROUPS)]
         sums = [keep.tile([P, n, M], F32, name="sums%d" % i) for i, (b, n) in enumerate(GROUPS)]
-        e_banks = (0, 1, 2, 0, 1)
-        u_banks = (0, 1, 2, 3, 4)
-        e_psum = [psum.tile([P, n, M], F32, name="e%d" % i, tag="e_bank%d" % e_banks[i]) for i, (b, n) in enumerate(GROUPS)]
-        u_psum = [psum.tile([P, n, M], F32, name="u%d" % i, tag="u_bank%d" % u_banks[i])[:] for i, (b, n) in enumerate(GROUPS)]
-        w4_plane = planes[:].bitcast(U8)
-        w8_plane = planes[ROWS:, :].bitcast(U8)
+        e_psum = [psum.tile([P, n, M], F32, name="e%d" % i) for i, (b, n) in enumerate(GROUPS)]
+        u_psum = [psum.tile([P, n, M], F32, name="u%d" % i)[:] for i, (b, n) in enumerate(GROUPS)]
+        w4_plane = w4_planes[:].bitcast(U8)
+        w8_plane = w8_planes[:]
 
         tab_scale_rows = tab[0, TABLE_WORD_BYTES:].rearrange("(b t) -> b t", t=T).bitcast(I32)
         w4_scale_rows = w4_scales[0].bitcast(I32)
 
+        warm_in = keep.tile([P, 1], F32, name="warm_in")
+        warm_out = keep.tile([P, 1], F32, name="warm_out")
+        nc.gpsimd.memset(warm_in[:], 0.0)
+        nc.scalar.activation(warm_out[:], warm_in[:], SILU)
+
+        nc.vector.memset(w4_planes[:], 0)
         nc.vector.memset(tab_scales[:STAGED, :], 0)
         for h in range(2):
             nc.vector.memset(token_planes[h][:], 0)
 
+        word_rows = tab[0, :TABLE_WORD_BYTES].rearrange("(p t) -> p t", p=P).bitcast(I32)
         nc.sync.dma_start(out=tab_scales[STAGED:, :], in_=tab_scale_rows)
         nc.sync.dma_start(out=lists[:], in_=offs)
+        nc.sync.dma_start(out=tab_words[:, :HEAD], in_=word_rows[:, :HEAD])
+        for q in range(QUADRANTS):
+            nc.sync.dma_start(out=w4_planes[32 * q : 32 * q + ROWS, :], in_=w4_scale_rows[ROWS * q : ROWS * (q + 1), :])
+        nc.sync.dma_start(out=tab_words[:, HEAD:], in_=word_rows[:, HEAD:])
         nc.sync.dma_start(out=w8_raw[:], in_=w8.rearrange("(p j) n -> p j n", j=PACK))
-        word_rows = tab[0, :TABLE_WORD_BYTES].rearrange("(p t) -> p t", p=P).bitcast(I32)
-        for q in range(1, QUADRANTS):
-            nc.sync.dma_start(out=planes[32 * q : 32 * q + ROWS, :], in_=w4_scale_rows[ROWS * q : ROWS * (q + 1), :])
-        nc.sync.dma_start(out=tab_words[:], in_=word_rows)
-        nc.sync.dma_start(out=planes[:ROWS, :], in_=w4_scale_rows[:ROWS, :])
         nc.sync.dma_start(out=w4_codes[:].bitcast(I32), in_=w4_words[0].bitcast(I32))
 
-        nc.scalar.copy(
-            out=w8_grouped[:].rearrange("p (c i) j -> p c j i", i=4),
-            in_=w8_raw[:].rearrange("p j (c i) -> p c j i", i=4),
-        )
         for h in range(2):
             offsets = lists[:, h * HALF // 16 : (h + 1) * HALF // 16]
             nc.vector.tensor_copy(out=picked_scales[h][:], in_=tab_scales[:].bitcast(U8).indirect(offsets))
-        nc.vector.quantize_mx(
-            out=w8_codes[:].bitcast(E4M3_X4),
-            scales=w8_plane,
-            in_=w8_grouped[:].rearrange("p n j -> p (n j)"),
-        )
         for h in range(2):
             for q in range(QUADRANTS):
                 nc.sync.dma_start(
                     out=token_planes[h][32 * q : 32 * q + ROWS, :],
                     in_=picked_scales[h][:].bitcast(I32)[STAGED + ROWS * q : STAGED + ROWS * (q + 1), :],
                 )
+        for h in range(2):
             nc.sync.dma_start(out=res[h][:], in_=r[h * HALF : (h + 1) * HALF, :].rearrange("(b p) n -> p b n", p=P))
+        nc.scalar.copy(
+            out=w8_grouped[:].rearrange("p (c i) j -> p c j i", i=4),
+            in_=w8_raw[:].rearrange("p j (c i) -> p c j i", i=4),
+        )
 
         def gather(g):
             width = GATHER_BLOCKS * P // 16
@@ -136,22 +137,27 @@ def tile_list_tabglu_tm_res_kernel(tc, tab, w4_words, w4_scales, w8, r, offs, ou
             rows = out[first * P : (first + count) * P, :]
             nc.sync.dma_start(out=rows.rearrange("(b p) n -> p b n", p=P), in_=sums[i][:])
 
-        for g in range(GATHERS):
+        for g in range(GATHERS - 1):
             gather(g)
-        for i in range(3):
-            gate(i)
-            up(i)
+        nc.vector.quantize_mx(
+            out=w8_codes[:].bitcast(E4M3_X4),
+            scales=w8_plane,
+            in_=w8_grouped[:].rearrange("p n j -> p (n j)"),
+        )
+        gather(GATHERS - 1)
+        gate(0)
+        gate(1)
+        up(0)
+        up(1)
+        gate(2)
+        up(2)
         gate(3)
-        gate(4)
         up(3)
-        up(4)
         product(0)
         product(1)
         finish(0, nc.vector)
         finish(1, nc.gpsimd)
         product(2)
         product(3)
-        product(4)
         finish(2, nc.vector)
         finish(3, nc.vector)
-        finish(4, nc.vector)

@@ -54,7 +54,9 @@ def tile_list_tabglu_tm_res_kernel(tc, tab, w4_words, w4_scales, w8, r, offs, ou
         picked_words.append(reuse.tile([P, GATHER_BLOCKS * P], U32, name="picked_last", align_bytes=64, offset=0))
         picked_scales = [keep.tile([P, HALF], U8, name="picked_scales%d" % h, align_bytes=64) for h in range(2)]
         token_planes = [keep.tile([P, HALF // 4], I32, name="token_planes%d" % h, align_bytes=64) for h in range(2)]
-        res = [keep.tile([P, HALF // P, M], F32, name="res%d" % h, align_bytes=64) for h in range(2)]
+        res_first = keep.tile([P, 2, M], F32, name="res_first", align_bytes=64)
+        res_rest = keep.tile([P, S // P - 2, M], F32, name="res_rest", align_bytes=64)
+        res = [res_first[:]] + [res_rest[:, b - 2 : b - 2 + n, :] for b, n in GROUPS[1:]]
         gates = [keep.tile([P, n, M], F32, name="gates%d" % i) for i, (b, n) in enumerate(GROUPS)]
         prods = [keep.tile([P, n, M], F32, name="prods%d" % i) for i, (b, n) in enumerate(GROUPS)]
         sums = [keep.tile([P, n, M], F32, name="sums%d" % i) for i, (b, n) in enumerate(GROUPS)]
@@ -66,25 +68,27 @@ def tile_list_tabglu_tm_res_kernel(tc, tab, w4_words, w4_scales, w8, r, offs, ou
         tab_scale_rows = tab[0, TABLE_WORD_BYTES:].rearrange("(b t) -> b t", t=T).bitcast(I32)
         w4_scale_rows = w4_scales[0].bitcast(I32)
 
-        warm_in = keep.tile([P, 1], F32, name="warm_in")
-        warm_out = keep.tile([P, 1], F32, name="warm_out")
-        nc.gpsimd.memset(warm_in[:], 0.0)
-        nc.scalar.activation(warm_out[:], warm_in[:], SILU)
-
         nc.vector.memset(w4_planes[:], 0)
         nc.vector.memset(tab_scales[:STAGED, :], 0)
         for h in range(2):
             nc.vector.memset(token_planes[h][:], 0)
 
         word_rows = tab[0, :TABLE_WORD_BYTES].rearrange("(p t) -> p t", p=P).bitcast(I32)
-        nc.sync.dma_start(out=tab_scales[STAGED:, :], in_=tab_scale_rows)
+        nc.scalar.dma_start(out=tab_scales[STAGED:, :], in_=tab_scale_rows)
         nc.sync.dma_start(out=lists[:], in_=offs)
+
+        warm_in = keep.tile([P, 1], F32, name="warm_in")
+        warm_out = keep.tile([P, 1], F32, name="warm_out")
+        nc.gpsimd.memset(warm_in[:], 0.0)
+        nc.scalar.activation(warm_out[:], warm_in[:], SILU)
+
         nc.sync.dma_start(out=tab_words[:, :HEAD], in_=word_rows[:, :HEAD])
         for q in range(QUADRANTS):
             nc.sync.dma_start(out=w4_planes[32 * q : 32 * q + ROWS, :], in_=w4_scale_rows[ROWS * q : ROWS * (q + 1), :])
         nc.sync.dma_start(out=tab_words[:, HEAD:], in_=word_rows[:, HEAD:])
         nc.sync.dma_start(out=w8_raw[:], in_=w8.rearrange("(p j) n -> p j n", j=PACK))
         nc.sync.dma_start(out=w4_codes[:].bitcast(I32), in_=w4_words[0].bitcast(I32))
+        nc.sync.dma_start(out=res_first[:], in_=r[: 2 * P, :].rearrange("(b p) n -> p b n", p=P))
 
         for h in range(2):
             offsets = lists[:, h * HALF // 16 : (h + 1) * HALF // 16]
@@ -95,8 +99,7 @@ def tile_list_tabglu_tm_res_kernel(tc, tab, w4_words, w4_scales, w8, r, offs, ou
                     out=token_planes[h][32 * q : 32 * q + ROWS, :],
                     in_=picked_scales[h][:].bitcast(I32)[STAGED + ROWS * q : STAGED + ROWS * (q + 1), :],
                 )
-        for h in range(2):
-            nc.sync.dma_start(out=res[h][:], in_=r[h * HALF : (h + 1) * HALF, :].rearrange("(b p) n -> p b n", p=P))
+        nc.sync.dma_start(out=res_rest[:], in_=r[2 * P :, :].rearrange("(b p) n -> p b n", p=P))
         nc.scalar.copy(
             out=w8_grouped[:].rearrange("p (c i) j -> p c j i", i=4),
             in_=w8_raw[:].rearrange("p j (c i) -> p c j i", i=4),
@@ -133,7 +136,7 @@ def tile_list_tabglu_tm_res_kernel(tc, tab, w4_words, w4_scales, w8, r, offs, ou
 
         def finish(i, adder):
             first, count = GROUPS[i]
-            adder.tensor_tensor(sums[i][:], prods[i][:], res[first * P // HALF][:, first % 4 : first % 4 + count, :], ADD)
+            adder.tensor_tensor(sums[i][:], prods[i][:], res[i], ADD)
             rows = out[first * P : (first + count) * P, :]
             nc.sync.dma_start(out=rows.rearrange("(b p) n -> p b n", p=P), in_=sums[i][:])
 
@@ -150,8 +153,8 @@ def tile_list_tabglu_tm_res_kernel(tc, tab, w4_words, w4_scales, w8, r, offs, ou
         up(0)
         up(1)
         gate(2)
-        up(2)
         gate(3)
+        up(2)
         up(3)
         product(0)
         product(1)

@@ -76,12 +76,6 @@ def tile_list_tabglu_tm_res_kernel(tc, tab, w4_words, w4_scales, w8, r, offs, ou
         word_rows = tab[0, :TABLE_WORD_BYTES].rearrange("(p t) -> p t", p=P).bitcast(I32)
         nc.scalar.dma_start(out=tab_scales[STAGED:, :], in_=tab_scale_rows)
         nc.sync.dma_start(out=lists[:], in_=offs)
-
-        warm_in = keep.tile([P, 1], F32, name="warm_in")
-        warm_out = keep.tile([P, 1], F32, name="warm_out")
-        nc.gpsimd.memset(warm_in[:], 0.0)
-        nc.scalar.activation(warm_out[:], warm_in[:], SILU)
-
         nc.sync.dma_start(out=tab_words[:, :HEAD], in_=word_rows[:, :HEAD])
         for q in range(QUADRANTS):
             nc.sync.dma_start(out=w4_planes[32 * q : 32 * q + ROWS, :], in_=w4_scale_rows[ROWS * q : ROWS * (q + 1), :])
@@ -100,10 +94,7 @@ def tile_list_tabglu_tm_res_kernel(tc, tab, w4_words, w4_scales, w8, r, offs, ou
                     in_=picked_scales[h][:].bitcast(I32)[STAGED + ROWS * q : STAGED + ROWS * (q + 1), :],
                 )
         nc.sync.dma_start(out=res_rest[:], in_=r[2 * P :, :].rearrange("(b p) n -> p b n", p=P))
-        nc.scalar.copy(
-            out=w8_grouped[:].rearrange("p (c i) j -> p c j i", i=4),
-            in_=w8_raw[:].rearrange("p j (c i) -> p c j i", i=4),
-        )
+        nc.gpsimd.tensor_scalar(w8_grouped[:], w8_raw[:].rearrange("p j n -> p n j"), 1.0, 0.0, MULT, ADD)
 
         def gather(g):
             width = GATHER_BLOCKS * P // 16

@@ -14,7 +14,7 @@ GATHER_BLOCKS = 2
 HALF = S // 2
 STAGED = P - ROWS * QUADRANTS
 GATHERS = S // (GATHER_BLOCKS * P)
-HEAD = 768
+HEAD = 640
 
 GROUPS = ((0, 2), (2, 2), (4, 2), (6, 2))
 

@@ -9,14 +9,12 @@ P = 128
 PACK = 4
 QUADRANTS = 4
 ROWS = 4
+LIST_ROWS = 16
 TABLE_WORD_BYTES = PACK * P * T
-GATHER_BLOCKS = 2
-HALF = S // 2
 STAGED = P - ROWS * QUADRANTS
-GATHERS = S // (GATHER_BLOCKS * P)
-HEAD = 640
-
-GROUPS = ((0, 2), (2, 2), (4, 2), (6, 2))
+HALF = S // 2
+PAIR = 2
+PAIRS = S // (PAIR * P)
 
 F32 = mybir.dt.float32
 BF16 = mybir.dt.bfloat16
@@ -35,40 +33,34 @@ def tile_list_tabglu_tm_res_kernel(tc, tab, w4_words, w4_scales, w8, r, offs, ou
     nc = tc.nc
     with ExitStack() as ctx:
         keep = ctx.enter_context(tc.tile_pool(name="keep", bufs=1))
-        reuse = ctx.enter_context(tc.tile_pool(name="reuse", bufs=1))
         psum = ctx.enter_context(tc.psum_pool(name="psum", bufs=1))
 
-        lists = keep.tile([P, S // 16], U16, name="lists")
+        lists = keep.tile([P, S // LIST_ROWS], U16, name="lists")
         tab_words = keep.tile([P, T], I32, name="tab_words", align_bytes=64)
         tab_scales = keep.tile([P, T // 4], I32, name="tab_scales", align_bytes=64)
         w4_codes = keep.tile([P, 2 * M], U8, name="w4_codes", align_bytes=64)
-        w4_planes = keep.tile([P, M // 4], I32, name="w4_planes", align_bytes=64)
-        w8_planes = keep.tile([P, M], U8, name="w8_planes", align_bytes=64)
-        w8_raw = reuse.tile([P, PACK, M], F32, name="w8_raw", align_bytes=64, offset=0)
+        w4_plane = keep.tile([P, M // 4], I32, name="w4_planes", align_bytes=64)
+        w8_plane = keep.tile([P, M], U8, name="w8_planes", align_bytes=64)
+        w8_raw = keep.tile([P, PACK, M], F32, name="w8_raw", align_bytes=64)
         w8_grouped = keep.tile([P, M, PACK], BF16, name="w8_grouped", align_bytes=64)
         w8_codes = keep.tile([P, M], U32, name="w8_codes", align_bytes=64)
-        picked_words = [
-            keep.tile([P, GATHER_BLOCKS * P], U32, name="picked_words%d" % g, align_bytes=64)
-            for g in range(GATHERS - 1)
-        ]
-        picked_words.append(reuse.tile([P, GATHER_BLOCKS * P], U32, name="picked_last", align_bytes=64, offset=0))
+        picked_words = [keep.tile([P, PAIR * P], U32, name="picked_words%d" % i, align_bytes=64) for i in range(PAIRS)]
         picked_scales = [keep.tile([P, HALF], U8, name="picked_scales%d" % h, align_bytes=64) for h in range(2)]
         token_planes = [keep.tile([P, HALF // 4], I32, name="token_planes%d" % h, align_bytes=64) for h in range(2)]
-        res_first = keep.tile([P, 2, M], F32, name="res_first", align_bytes=64)
-        res_rest = keep.tile([P, S // P - 2, M], F32, name="res_rest", align_bytes=64)
-        res = [res_first[:]] + [res_rest[:, b - 2 : b - 2 + n, :] for b, n in GROUPS[1:]]
-        gates = [keep.tile([P, n, M], F32, name="gates%d" % i) for i, (b, n) in enumerate(GROUPS)]
-        prods = [keep.tile([P, n, M], F32, name="prods%d" % i) for i, (b, n) in enumerate(GROUPS)]
-        sums = [keep.tile([P, n, M], F32, name="sums%d" % i) for i, (b, n) in enumerate(GROUPS)]
-        e_psum = [psum.tile([P, n, M], F32, name="e%d" % i) for i, (b, n) in enumerate(GROUPS)]
-        u_psum = [psum.tile([P, n, M], F32, name="u%d" % i)[:] for i, (b, n) in enumerate(GROUPS)]
-        w4_plane = w4_planes[:].bitcast(U8)
-        w8_plane = w8_planes[:]
+        res_first = keep.tile([P, PAIR, M], F32, name="res_first", align_bytes=64)
+        res_second = keep.tile([P, PAIR, M], F32, name="res_second", align_bytes=64)
+        res_rest = keep.tile([P, 2 * PAIR, M], F32, name="res_rest", align_bytes=64)
+        res = [res_first[:], res_second[:], res_rest[:, :PAIR, :], res_rest[:, PAIR:, :]]
+        gates = [keep.tile([P, PAIR, M], F32, name="gates%d" % i) for i in range(PAIRS)]
+        prods = [keep.tile([P, PAIR, M], F32, name="prods%d" % i) for i in range(PAIRS)]
+        sums = [keep.tile([P, PAIR, M], F32, name="sums%d" % i) for i in range(PAIRS)]
+        e_psum = [psum.tile([P, PAIR, M], F32, name="e%d" % i) for i in range(PAIRS)]
+        u_psum = [psum.tile([P, PAIR, M], F32, name="u%d" % i) for i in range(PAIRS)]
 
         tab_scale_rows = tab[0, TABLE_WORD_BYTES:].rearrange("(b t) -> b t", t=T).bitcast(I32)
         w4_scale_rows = w4_scales[0].bitcast(I32)
 
-        nc.vector.memset(w4_planes[:], 0)
+        nc.vector.memset(w4_plane[:], 0)
         nc.vector.memset(tab_scales[:STAGED, :], 0)
         for h in range(2):
             nc.vector.memset(token_planes[h][:], 0)
@@ -76,16 +68,16 @@ def tile_list_tabglu_tm_res_kernel(tc, tab, w4_words, w4_scales, w8, r, offs, ou
         word_rows = tab[0, :TABLE_WORD_BYTES].rearrange("(p t) -> p t", p=P).bitcast(I32)
         nc.scalar.dma_start(out=tab_scales[STAGED:, :], in_=tab_scale_rows)
         nc.sync.dma_start(out=lists[:], in_=offs)
-        nc.sync.dma_start(out=tab_words[:, :HEAD], in_=word_rows[:, :HEAD])
-        for q in range(QUADRANTS):
-            nc.sync.dma_start(out=w4_planes[32 * q : 32 * q + ROWS, :], in_=w4_scale_rows[ROWS * q : ROWS * (q + 1), :])
-        nc.sync.dma_start(out=tab_words[:, HEAD:], in_=word_rows[:, HEAD:])
         nc.sync.dma_start(out=w8_raw[:], in_=w8.rearrange("(p j) n -> p j n", j=PACK))
+        for q in range(QUADRANTS):
+            if q == QUADRANTS - 1:
+                nc.sync.dma_start(out=tab_words[:], in_=word_rows)
+            nc.sync.dma_start(out=w4_plane[32 * q : 32 * q + ROWS, :], in_=w4_scale_rows[ROWS * q : ROWS * (q + 1), :])
         nc.sync.dma_start(out=w4_codes[:].bitcast(I32), in_=w4_words[0].bitcast(I32))
-        nc.sync.dma_start(out=res_first[:], in_=r[: 2 * P, :].rearrange("(b p) n -> p b n", p=P))
+        nc.sync.dma_start(out=res_first[:], in_=r[: PAIR * P, :].rearrange("(b p) n -> p b n", p=P))
 
         for h in range(2):
-            offsets = lists[:, h * HALF // 16 : (h + 1) * HALF // 16]
+            offsets = lists[:, h * HALF // LIST_ROWS : (h + 1) * HALF // LIST_ROWS]
             nc.vector.tensor_copy(out=picked_scales[h][:], in_=tab_scales[:].bitcast(U8).indirect(offsets))
         for h in range(2):
             for q in range(QUADRANTS):
@@ -93,22 +85,26 @@ def tile_list_tabglu_tm_res_kernel(tc, tab, w4_words, w4_scales, w8, r, offs, ou
                     out=token_planes[h][32 * q : 32 * q + ROWS, :],
                     in_=picked_scales[h][:].bitcast(I32)[STAGED + ROWS * q : STAGED + ROWS * (q + 1), :],
                 )
-        nc.sync.dma_start(out=res_rest[:], in_=r[2 * P :, :].rearrange("(b p) n -> p b n", p=P))
-        nc.gpsimd.tensor_scalar(w8_grouped[:], w8_raw[:].rearrange("p j n -> p n j"), 1.0, 0.0, MULT, ADD)
+        nc.sync.dma_start(out=res_second[:], in_=r[PAIR * P : HALF, :].rearrange("(b p) n -> p b n", p=P))
+        nc.sync.dma_start(out=res_rest[:], in_=r[HALF:, :].rearrange("(b p) n -> p b n", p=P))
 
-        def gather(g):
-            width = GATHER_BLOCKS * P // 16
-            offsets = lists[:, g * width : (g + 1) * width]
-            nc.vector.tensor_copy(out=picked_words[g][:], in_=tab_words[:].bitcast(U32).indirect(offsets))
+        nc.scalar.copy(
+            out=w8_grouped[:].rearrange("p (c i) j -> p c j i", i=4),
+            in_=w8_raw[:].rearrange("p j (c i) -> p c j i", i=4),
+        )
+
+        def gather(i):
+            width = PAIR * P // LIST_ROWS
+            offsets = lists[:, i * width : (i + 1) * width]
+            nc.vector.tensor_copy(out=picked_words[i][:], in_=tab_words[:].bitcast(U32).indirect(offsets))
 
         def multiply(bank, i, weights, weight_scales):
-            first, count = GROUPS[i]
-            for b in range(first, first + count):
-                at = b % GATHER_BLOCKS * P
+            for j in range(PAIR):
+                half, at = divmod((PAIR * i + j) * P, HALF)
                 nc.tensor.matmul_mx(
-                    out=bank[:, b - first, :],
-                    lhsT=picked_words[b // GATHER_BLOCKS][:, at : at + P].bitcast(E4M3_X4),
-                    lhsT_scale=token_planes[b * P // HALF][:].bitcast(U8)[:, b * P % HALF : b * P % HALF + P],
+                    out=bank[:, j, :],
+                    lhsT=picked_words[i][:, j * P : (j + 1) * P].bitcast(E4M3_X4),
+                    lhsT_scale=token_planes[half][:].bitcast(U8)[:, at : at + P],
                     rhs=weights,
                     rhs_scale=weight_scales,
                     start=True,
@@ -116,37 +112,37 @@ def tile_list_tabglu_tm_res_kernel(tc, tab, w4_words, w4_scales, w8, r, offs, ou
                 )
 
         def gate(i):
-            multiply(e_psum[i][:], i, w4_codes[:].bitcast(E2M1_X4), w4_plane)
+            multiply(e_psum[i][:], i, w4_codes[:].bitcast(E2M1_X4), w4_plane[:].bitcast(U8))
             nc.scalar.activation(gates[i][:], e_psum[i][:], SILU)
 
         def up(i):
-            multiply(u_psum[i], i, w8_codes[:].bitcast(E4M3_X4), w8_plane)
+            multiply(u_psum[i][:], i, w8_codes[:].bitcast(E4M3_X4), w8_plane[:])
 
         def product(i):
-            nc.vector.tensor_tensor(prods[i][:], gates[i][:], u_psum[i], MULT)
+            nc.vector.tensor_tensor(prods[i][:], gates[i][:], u_psum[i][:], MULT)
 
         def finish(i, adder):
-            first, count = GROUPS[i]
             adder.tensor_tensor(sums[i][:], prods[i][:], res[i], ADD)
-            rows = out[first * P : (first + count) * P, :]
+            rows = out[PAIR * i * P : PAIR * (i + 1) * P, :]
             nc.sync.dma_start(out=rows.rearrange("(b p) n -> p b n", p=P), in_=sums[i][:])
 
-        for g in range(GATHERS - 1):
-            gather(g)
         nc.vector.quantize_mx(
             out=w8_codes[:].bitcast(E4M3_X4),
-            scales=w8_plane,
+            scales=w8_plane[:],
             in_=w8_grouped[:].rearrange("p n j -> p (n j)"),
         )
-        gather(GATHERS - 1)
+        for i in range(PAIRS):
+            gather(i)
+
         gate(0)
-        gate(1)
         up(0)
+        gate(1)
         up(1)
         gate(2)
         gate(3)
         up(2)
         up(3)
+
         product(0)
         product(1)
         finish(0, nc.vector)

@@ -15,6 +15,7 @@ STAGED = P - ROWS * QUADRANTS
 HALF = S // 2
 PAIR = 2
 PAIRS = S // (PAIR * P)
+HEAD = 640
 
 F32 = mybir.dt.float32
 BF16 = mybir.dt.bfloat16
@@ -34,6 +35,7 @@ def tile_list_tabglu_tm_res_kernel(tc, tab, w4_words, w4_scales, w8, r, offs, ou
     with ExitStack() as ctx:
         keep = ctx.enter_context(tc.tile_pool(name="keep", bufs=1))
         psum = ctx.enter_context(tc.psum_pool(name="psum", bufs=1))
+        twice = ctx.enter_context(tc.tile_pool(name="twice", bufs=1))
 
         lists = keep.tile([P, S // LIST_ROWS], U16, name="lists")
         tab_words = keep.tile([P, T], I32, name="tab_words", align_bytes=64)
@@ -41,10 +43,15 @@ def tile_list_tabglu_tm_res_kernel(tc, tab, w4_words, w4_scales, w8, r, offs, ou
         w4_codes = keep.tile([P, 2 * M], U8, name="w4_codes", align_bytes=64)
         w4_plane = keep.tile([P, M // 4], I32, name="w4_planes", align_bytes=64)
         w8_plane = keep.tile([P, M], U8, name="w8_planes", align_bytes=64)
-        w8_raw = keep.tile([P, PACK, M], F32, name="w8_raw", align_bytes=64)
+        w8_raw = twice.tile([P, PACK, M], F32, name="w8_raw", align_bytes=64, offset=0)
         w8_grouped = keep.tile([P, M, PACK], BF16, name="w8_grouped", align_bytes=64)
         w8_codes = keep.tile([P, M], U32, name="w8_codes", align_bytes=64)
-        picked_words = [keep.tile([P, PAIR * P], U32, name="picked_words%d" % i, align_bytes=64) for i in range(PAIRS)]
+        picked_words = [keep.tile([P, PAIR * P], U32, name="picked_words%d" % i, align_bytes=64) for i in range(2)]
+        picked_words.extend(
+            twice.tile([P, PAIR * P], U32, name="picked_late%d" % i, align_bytes=64, offset=i * 4 * PAIR * P)
+            for i in range(2)
+        )
+        warm = keep.tile([P, 2], F32, name="warm")
         picked_scales = [keep.tile([P, HALF], U8, name="picked_scales%d" % h, align_bytes=64) for h in range(2)]
         token_planes = [keep.tile([P, HALF // 4], I32, name="token_planes%d" % h, align_bytes=64) for h in range(2)]
         res_first = keep.tile([P, PAIR, M], F32, name="res_first", align_bytes=64)
@@ -53,7 +60,9 @@ def tile_list_tabglu_tm_res_kernel(tc, tab, w4_words, w4_scales, w8, r, offs, ou
         res = [res_first[:], res_second[:], res_rest[:, :PAIR, :], res_rest[:, PAIR:, :]]
         gates = [keep.tile([P, PAIR, M], F32, name="gates%d" % i) for i in range(PAIRS)]
         prods = [keep.tile([P, PAIR, M], F32, name="prods%d" % i) for i in range(PAIRS)]
-        sums = [keep.tile([P, PAIR, M], F32, name="sums%d" % i) for i in range(PAIRS)]
+        sums_first = keep.tile([P, 2, PAIR, M], F32, name="sums_first")
+        sums = [sums_first[:, 0, :, :], sums_first[:, 1, :, :]]
+        sums.extend(keep.tile([P, PAIR, M], F32, name="sums%d" % i)[:] for i in range(2, PAIRS))
         e_psum = [psum.tile([P, PAIR, M], F32, name="e%d" % i) for i in range(PAIRS)]
         u_psum = [psum.tile([P, PAIR, M], F32, name="u%d" % i) for i in range(PAIRS)]
 
@@ -61,6 +70,8 @@ def tile_list_tabglu_tm_res_kernel(tc, tab, w4_words, w4_scales, w8, r, offs, ou
         w4_scale_rows = w4_scales[0].bitcast(I32)
 
         nc.vector.memset(w4_plane[:], 0)
+        nc.gpsimd.memset(warm[:, 0:1], 0.0)
+        nc.scalar.activation(warm[:, 1:2], warm[:, 0:1], SILU)
         nc.vector.memset(tab_scales[:STAGED, :], 0)
         for h in range(2):
             nc.vector.memset(token_planes[h][:], 0)
@@ -68,25 +79,25 @@ def tile_list_tabglu_tm_res_kernel(tc, tab, w4_words, w4_scales, w8, r, offs, ou
         word_rows = tab[0, :TABLE_WORD_BYTES].rearrange("(p t) -> p t", p=P).bitcast(I32)
         nc.scalar.dma_start(out=tab_scales[STAGED:, :], in_=tab_scale_rows)
         nc.sync.dma_start(out=lists[:], in_=offs)
-        nc.sync.dma_start(out=w8_raw[:], in_=w8.rearrange("(p j) n -> p j n", j=PACK))
+        nc.sync.dma_start(out=tab_words[:, :HEAD], in_=word_rows[:, :HEAD])
         for q in range(QUADRANTS):
-            if q == QUADRANTS - 1:
-                nc.sync.dma_start(out=tab_words[:], in_=word_rows)
             nc.sync.dma_start(out=w4_plane[32 * q : 32 * q + ROWS, :], in_=w4_scale_rows[ROWS * q : ROWS * (q + 1), :])
+        nc.sync.dma_start(out=tab_words[:, HEAD:], in_=word_rows[:, HEAD:])
         nc.sync.dma_start(out=w4_codes[:].bitcast(I32), in_=w4_words[0].bitcast(I32))
-        nc.sync.dma_start(out=res_first[:], in_=r[: PAIR * P, :].rearrange("(b p) n -> p b n", p=P))
+        nc.sync.dma_start(out=w8_raw[:], in_=w8.rearrange("(p j) n -> p j n", j=PACK))
 
         for h in range(2):
             offsets = lists[:, h * HALF // LIST_ROWS : (h + 1) * HALF // LIST_ROWS]
-            nc.vector.tensor_copy(out=picked_scales[h][:], in_=tab_scales[:].bitcast(U8).indirect(offsets))
+            nc.vector.tensor_copy(out=picked_scales[h][:].rearrange("p (g j m) -> p g m j", j=PAIR, m=P), in_=tab_scales[:].bitcast(U8).indirect(offsets))
         for h in range(2):
             for q in range(QUADRANTS):
                 nc.sync.dma_start(
                     out=token_planes[h][32 * q : 32 * q + ROWS, :],
                     in_=picked_scales[h][:].bitcast(I32)[STAGED + ROWS * q : STAGED + ROWS * (q + 1), :],
                 )
-        nc.sync.dma_start(out=res_second[:], in_=r[PAIR * P : HALF, :].rearrange("(b p) n -> p b n", p=P))
-        nc.sync.dma_start(out=res_rest[:], in_=r[HALF:, :].rearrange("(b p) n -> p b n", p=P))
+        nc.sync.dma_start(out=res_first[:], in_=r[: PAIR * P, :].rearrange("(p b) n -> p b n", p=P))
+        nc.sync.dma_start(out=res_second[:], in_=r[PAIR * P : HALF, :].rearrange("(p b) n -> p b n", p=P))
+        nc.sync.dma_start(out=res_rest[:].rearrange("p (g b) n -> p g b n", b=PAIR), in_=r[HALF:, :].rearrange("(g p b) n -> p g b n", p=P, b=PAIR))
 
         nc.scalar.copy(
             out=w8_grouped[:].rearrange("p (c i) j -> p c j i", i=4),
@@ -96,7 +107,7 @@ def tile_list_tabglu_tm_res_kernel(tc, tab, w4_words, w4_scales, w8, r, offs, ou
         def gather(i):
             width = PAIR * P // LIST_ROWS
             offsets = lists[:, i * width : (i + 1) * width]
-            nc.vector.tensor_copy(out=picked_words[i][:], in_=tab_words[:].bitcast(U32).indirect(offsets))
+            nc.vector.tensor_copy(out=picked_words[i][:].rearrange("p (j m) -> p m j", j=PAIR), in_=tab_words[:].bitcast(U32).indirect(offsets))
 
         def multiply(bank, i, weights, weight_scales):
             for j in range(PAIR):
@@ -122,21 +133,25 @@ def tile_list_tabglu_tm_res_kernel(tc, tab, w4_words, w4_scales, w8, r, offs, ou
             nc.vector.tensor_tensor(prods[i][:], gates[i][:], u_psum[i][:], MULT)
 
         def finish(i, adder):
-            adder.tensor_tensor(sums[i][:], prods[i][:], res[i], ADD)
-            rows = out[PAIR * i * P : PAIR * (i + 1) * P, :]
-            nc.sync.dma_start(out=rows.rearrange("(b p) n -> p b n", p=P), in_=sums[i][:])
+            adder.tensor_tensor(sums[i], prods[i][:], res[i], ADD)
+            if i == 1:
+                nc.sync.dma_start(out=out[:HALF, :].rearrange("(g p b) n -> p g b n", p=P, b=PAIR), in_=sums_first[:])
+            if i > 1:
+                rows = out[PAIR * i * P : PAIR * (i + 1) * P, :]
+                nc.sync.dma_start(out=rows.rearrange("(p b) n -> p b n", p=P), in_=sums[i])
 
-        nc.vector.quantize_mx(
-            out=w8_codes[:].bitcast(E4M3_X4),
-            scales=w8_plane[:],
-            in_=w8_grouped[:].rearrange("p n j -> p (n j)"),
-        )
         for i in range(PAIRS):
+            if i == 2:
+                nc.vector.quantize_mx(
+                    out=w8_codes[:].bitcast(E4M3_X4),
+                    scales=w8_plane[:],
+                    in_=w8_grouped[:].rearrange("p n j -> p (n j)"),
+                )
             gather(i)
 
         gate(0)
-        up(0)
         gate(1)
+        up(0)
         up(1)
         gate(2)
         gate(3)

@@ -54,17 +54,15 @@ def tile_list_tabglu_tm_res_kernel(tc, tab, w4_words, w4_scales, w8, r, offs, ou
         warm = keep.tile([P, 2], F32, name="warm")
         picked_scales = [keep.tile([P, HALF], U8, name="picked_scales%d" % h, align_bytes=64) for h in range(2)]
         token_planes = [keep.tile([P, HALF // 4], I32, name="token_planes%d" % h, align_bytes=64) for h in range(2)]
-        res_first = keep.tile([P, PAIR, M], F32, name="res_first", align_bytes=64)
-        res_second = keep.tile([P, PAIR, M], F32, name="res_second", align_bytes=64)
+        res_first = keep.tile([P, 2 * PAIR, M], F32, name="res_first", align_bytes=64)
         res_rest = keep.tile([P, 2 * PAIR, M], F32, name="res_rest", align_bytes=64)
-        res = [res_first[:], res_second[:], res_rest[:, :PAIR, :], res_rest[:, PAIR:, :]]
+        res = [res_first[:, :PAIR, :], res_first[:, PAIR:, :], res_rest[:, :PAIR, :], res_rest[:, PAIR:, :]]
         gates = [keep.tile([P, PAIR, M], F32, name="gates%d" % i) for i in range(PAIRS)]
         prods = [keep.tile([P, PAIR, M], F32, name="prods%d" % i) for i in range(PAIRS)]
-        sums_first = keep.tile([P, 2, PAIR, M], F32, name="sums_first")
-        sums = [sums_first[:, 0, :, :], sums_first[:, 1, :, :]]
-        sums.extend(keep.tile([P, PAIR, M], F32, name="sums%d" % i)[:] for i in range(2, PAIRS))
-        e_psum = [psum.tile([P, PAIR, M], F32, name="e%d" % i) for i in range(PAIRS)]
-        u_psum = [psum.tile([P, PAIR, M], F32, name="u%d" % i) for i in range(PAIRS)]
+        sums = [keep.tile([P, PAIR, M], F32, name="sums%d" % i) for i in range(PAIRS)]
+        banks = [psum.tile([P, PAIR, M], F32, name="bank%d" % i) for i in range(8)]
+        e_at = [(0, 0), (0, 1), (2, 0), (2, 1), (4, 0), (5, 0), (0, 0), (2, 0)]
+        u_at = [(1, 0), (1, 1), (3, 0), (3, 1), (6, 0), (6, 1), (7, 0), (1, 0)]
 
         tab_scale_rows = tab[0, TABLE_WORD_BYTES:].rearrange("(b t) -> b t", t=T).bitcast(I32)
         w4_scale_rows = w4_scales[0].bitcast(I32)
@@ -95,8 +93,7 @@ def tile_list_tabglu_tm_res_kernel(tc, tab, w4_words, w4_scales, w8, r, offs, ou
                     out=token_planes[h][32 * q : 32 * q + ROWS, :],
                     in_=picked_scales[h][:].bitcast(I32)[STAGED + ROWS * q : STAGED + ROWS * (q + 1), :],
                 )
-        nc.sync.dma_start(out=res_first[:], in_=r[: PAIR * P, :].rearrange("(p b) n -> p b n", p=P))
-        nc.sync.dma_start(out=res_second[:], in_=r[PAIR * P : HALF, :].rearrange("(p b) n -> p b n", p=P))
+        nc.sync.dma_start(out=res_first[:].rearrange("p (g b) n -> p g b n", b=PAIR), in_=r[:HALF, :].rearrange("(g p b) n -> p g b n", p=P, b=PAIR))
         nc.sync.dma_start(out=res_rest[:].rearrange("p (g b) n -> p g b n", b=PAIR), in_=r[HALF:, :].rearrange("(g p b) n -> p g b n", p=P, b=PAIR))
 
         nc.scalar.copy(
@@ -109,36 +106,43 @@ def tile_list_tabglu_tm_res_kernel(tc, tab, w4_words, w4_scales, w8, r, offs, ou
             offsets = lists[:, i * width : (i + 1) * width]
             nc.vector.tensor_copy(out=picked_words[i][:].rearrange("p (j m) -> p m j", j=PAIR), in_=tab_words[:].bitcast(U32).indirect(offsets))
 
-        def multiply(bank, i, weights, weight_scales):
-            for j in range(PAIR):
-                half, at = divmod((PAIR * i + j) * P, HALF)
-                nc.tensor.matmul_mx(
-                    out=bank[:, j, :],
-                    lhsT=picked_words[i][:, j * P : (j + 1) * P].bitcast(E4M3_X4),
-                    lhsT_scale=token_planes[half][:].bitcast(U8)[:, at : at + P],
-                    rhs=weights,
-                    rhs_scale=weight_scales,
-                    start=True,
-                    stop=True,
-                )
+        def psum_of(at, b, n):
+            bank, place = at[b]
+            return banks[bank][:, place : place + n, :]
 
-        def gate(i):
-            multiply(e_psum[i][:], i, w4_codes[:].bitcast(E2M1_X4), w4_plane[:].bitcast(U8))
-            nc.scalar.activation(gates[i][:], e_psum[i][:], SILU)
+        def part(tiles, b, n):
+            return tiles[b // PAIR][:, b % PAIR : b % PAIR + n, :]
 
-        def up(i):
-            multiply(u_psum[i][:], i, w8_codes[:].bitcast(E4M3_X4), w8_plane[:])
+        def multiply(at, b, weights, weight_scales):
+            half, column = divmod(b * P, HALF)
+            nc.tensor.matmul_mx(
+                out=psum_of(at, b, 1)[:, 0, :],
+                lhsT=picked_words[b // PAIR][:, b % PAIR * P : (b % PAIR + 1) * P].bitcast(E4M3_X4),
+                lhsT_scale=token_planes[half][:].bitcast(U8)[:, column : column + P],
+                rhs=weights,
+                rhs_scale=weight_scales,
+                start=True,
+                stop=True,
+            )
 
-        def product(i):
-            nc.vector.tensor_tensor(prods[i][:], gates[i][:], u_psum[i][:], MULT)
+        def gate(b, n):
+            for j in range(n):
+                multiply(e_at, b + j, w4_codes[:].bitcast(E2M1_X4), w4_plane[:].bitcast(U8))
+            nc.scalar.activation(part(gates, b, n), psum_of(e_at, b, n), SILU)
 
-        def finish(i, adder):
-            adder.tensor_tensor(sums[i], prods[i][:], res[i], ADD)
-            if i == 1:
-                nc.sync.dma_start(out=out[:HALF, :].rearrange("(g p b) n -> p g b n", p=P, b=PAIR), in_=sums_first[:])
-            if i > 1:
-                rows = out[PAIR * i * P : PAIR * (i + 1) * P, :]
-                nc.sync.dma_start(out=rows.rearrange("(p b) n -> p b n", p=P), in_=sums[i])
+        def up(b, n):
+            for j in range(n):
+                multiply(u_at, b + j, w8_codes[:].bitcast(E4M3_X4), w8_plane[:])
+
+        def product(b, n):
+            nc.vector.tensor_tensor(part(prods, b, n), part(gates, b, n), psum_of(u_at, b, n), MULT)
+
+        def add(adder, b, n):
+            adder.tensor_tensor(part(sums, b, n), part(prods, b, n), part(res, b, n), ADD)
+
+        def store(i):
+            rows = out[PAIR * i * P : PAIR * (i + 1) * P, :]
+            nc.sync.dma_start(out=rows.rearrange("(p b) n -> p b n", p=P), in_=sums[i][:])
 
         for i in range(PAIRS):
             if i == 2:
@@ -149,20 +153,30 @@ def tile_list_tabglu_tm_res_kernel(tc, tab, w4_words, w4_scales, w8, r, offs, ou
                 )
             gather(i)
 
-        gate(0)
-        gate(1)
-        up(0)
-        up(1)
-        gate(2)
-        gate(3)
-        up(2)
-        up(3)
+        gate(0, 2)
+        gate(2, 2)
+        up(0, 2)
+        up(2, 2)
+        product(0, 2)
+        product(2, 2)
+        add(nc.vector, 0, 2)
+        store(0)
+        add(nc.vector, 2, 1)
+        add(nc.gpsimd, 3, 1)
+        store(1)
 
-        product(0)
-        product(1)
-        finish(0, nc.vector)
-        finish(1, nc.gpsimd)
-        product(2)
-        product(3)
-        finish(2, nc.vector)
-        finish(3, nc.vector)
+        gate(4, 1)
+        gate(5, 1)
+        up(4, 1)
+        gate(6, 1)
+        up(5, 1)
+        gate(7, 1)
+        up(6, 1)
+        up(7, 1)
+        product(4, 2)
+        product(6, 1)
+        product(7, 1)
+        add(nc.vector, 4, 2)
+        store(2)
+        add(nc.vector, 6, 2)
+        store(3)

@@ -15,6 +15,7 @@ STAGED = P - ROWS * QUADRANTS
 HALF = S // 2
 PAIR = 2
 PAIRS = S // (PAIR * P)
+SHARE = 96
 HEAD = 640
 
 F32 = mybir.dt.float32
@@ -81,8 +82,8 @@ def tile_list_tabglu_tm_res_kernel(tc, tab, w4_words, w4_scales, w8, r, offs, ou
         for q in range(QUADRANTS):
             nc.sync.dma_start(out=w4_plane[32 * q : 32 * q + ROWS, :], in_=w4_scale_rows[ROWS * q : ROWS * (q + 1), :])
         nc.sync.dma_start(out=tab_words[:, HEAD:], in_=word_rows[:, HEAD:])
-        nc.sync.dma_start(out=w4_codes[:].bitcast(I32), in_=w4_words[0].bitcast(I32))
         nc.sync.dma_start(out=w8_raw[:], in_=w8.rearrange("(p j) n -> p j n", j=PACK))
+        nc.sync.dma_start(out=w4_codes[:].bitcast(I32), in_=w4_words[0].bitcast(I32))
 
         for h in range(2):
             offsets = lists[:, h * HALF // LIST_ROWS : (h + 1) * HALF // LIST_ROWS]
@@ -97,8 +98,16 @@ def tile_list_tabglu_tm_res_kernel(tc, tab, w4_words, w4_scales, w8, r, offs, ou
         nc.sync.dma_start(out=res_rest[:].rearrange("p (g b) n -> p g b n", b=PAIR), in_=r[HALF:, :].rearrange("(g p b) n -> p g b n", p=P, b=PAIR))
 
         nc.scalar.copy(
-            out=w8_grouped[:].rearrange("p (c i) j -> p c j i", i=4),
-            in_=w8_raw[:].rearrange("p j (c i) -> p c j i", i=4),
+            out=w8_grouped[:, :SHARE, :].rearrange("p (c i) j -> p c j i", i=4),
+            in_=w8_raw[:, :, :SHARE].rearrange("p j (c i) -> p c j i", i=4),
+        )
+        nc.gpsimd.tensor_scalar(
+            w8_grouped[:, SHARE:, :].rearrange("p (c i) j -> p c j i", i=4),
+            w8_raw[:, :, SHARE:].rearrange("p j (c i) -> p c j i", i=4),
+            1.0,
+            0.0,
+            MULT,
+            ADD,
         )
 
         def gather(i):

from contextlib import ExitStack

import concourse.mybir as mybir

K, M, T, S = 512, 128, 2048, 1024
FLOPS = 2 * 2 * K * M * S

P = 128
PACK = 4
QUADRANTS = 4
ROWS = 4
LIST_ROWS = 16
TABLE_WORD_BYTES = PACK * P * T
STAGED = P - ROWS * QUADRANTS
HALF = S // 2
PAIR = 2
PAIRS = S // (PAIR * P)
SHARE = 96
HEAD = 640

F32 = mybir.dt.float32
BF16 = mybir.dt.bfloat16
I32 = mybir.dt.int32
U32 = mybir.dt.uint32
U16 = mybir.dt.uint16
U8 = mybir.dt.uint8
E4M3_X4 = mybir.dt.float8_e4m3fn_x4
E2M1_X4 = mybir.dt.float4_e2m1fn_x4
SILU = mybir.ActivationFunctionType.Silu
MULT = mybir.AluOpType.mult
ADD = mybir.AluOpType.add


def tile_list_tabglu_tm_res_kernel(tc, tab, w4_words, w4_scales, w8, r, offs, out):
    nc = tc.nc
    with ExitStack() as ctx:
        keep = ctx.enter_context(tc.tile_pool(name="keep", bufs=1))
        psum = ctx.enter_context(tc.psum_pool(name="psum", bufs=1))
        twice = ctx.enter_context(tc.tile_pool(name="twice", bufs=1))

        lists = keep.tile([P, S // LIST_ROWS], U16, name="lists")
        tab_words = keep.tile([P, T], I32, name="tab_words", align_bytes=64)
        tab_scales = keep.tile([P, T // 4], I32, name="tab_scales", align_bytes=64)
        w4_codes = keep.tile([P, 2 * M], U8, name="w4_codes", align_bytes=64)
        w4_plane = keep.tile([P, M // 4], I32, name="w4_planes", align_bytes=64)
        w8_plane = keep.tile([P, M], U8, name="w8_planes", align_bytes=64)
        w8_raw = twice.tile([P, PACK, M], F32, name="w8_raw", align_bytes=64, offset=0)
        w8_grouped = keep.tile([P, M, PACK], BF16, name="w8_grouped", align_bytes=64)
        w8_codes = keep.tile([P, M], U32, name="w8_codes", align_bytes=64)
        picked_words = [keep.tile([P, PAIR * P], U32, name="picked_words%d" % i, align_bytes=64) for i in range(2)]
        picked_words.extend(
            twice.tile([P, PAIR * P], U32, name="picked_late%d" % i, align_bytes=64, offset=i * 4 * PAIR * P)
            for i in range(2)
        )
        warm = keep.tile([P, 2], F32, name="warm")
        picked_scales = [keep.tile([P, HALF], U8, name="picked_scales%d" % h, align_bytes=64) for h in range(2)]
        token_planes = [keep.tile([P, HALF // 4], I32, name="token_planes%d" % h, align_bytes=64) for h in range(2)]
        res_first = keep.tile([P, 2 * PAIR, M], F32, name="res_first", align_bytes=64)
        res_rest = keep.tile([P, 2 * PAIR, M], F32, name="res_rest", align_bytes=64)
        res = [res_first[:, :PAIR, :], res_first[:, PAIR:, :], res_rest[:, :PAIR, :], res_rest[:, PAIR:, :]]
        gates = [keep.tile([P, PAIR, M], F32, name="gates%d" % i) for i in range(PAIRS)]
        prods = [keep.tile([P, PAIR, M], F32, name="prods%d" % i) for i in range(PAIRS)]
        sums = [keep.tile([P, PAIR, M], F32, name="sums%d" % i) for i in range(PAIRS)]
        banks = [psum.tile([P, PAIR, M], F32, name="bank%d" % i) for i in range(8)]
        e_at = [(0, 0), (0, 1), (2, 0), (2, 1), (4, 0), (5, 0), (0, 0), (2, 0)]
        u_at = [(1, 0), (1, 1), (3, 0), (3, 1), (6, 0), (6, 1), (7, 0), (1, 0)]

        tab_scale_rows = tab[0, TABLE_WORD_BYTES:].rearrange("(b t) -> b t", t=T).bitcast(I32)
        w4_scale_rows = w4_scales[0].bitcast(I32)

        nc.vector.memset(w4_plane[:], 0)
        nc.gpsimd.memset(warm[:, 0:1], 0.0)
        nc.scalar.activation(warm[:, 1:2], warm[:, 0:1], SILU)
        nc.vector.memset(tab_scales[:STAGED, :], 0)
        for h in range(2):
            nc.vector.memset(token_planes[h][:], 0)

        word_rows = tab[0, :TABLE_WORD_BYTES].rearrange("(p t) -> p t", p=P).bitcast(I32)
        nc.scalar.dma_start(out=tab_scales[STAGED:, :], in_=tab_scale_rows)
        nc.sync.dma_start(out=lists[:], in_=offs)
        nc.sync.dma_start(out=tab_words[:, :HEAD], in_=word_rows[:, :HEAD])
        for q in range(QUADRANTS):
            nc.sync.dma_start(out=w4_plane[32 * q : 32 * q + ROWS, :], in_=w4_scale_rows[ROWS * q : ROWS * (q + 1), :])
        nc.sync.dma_start(out=tab_words[:, HEAD:], in_=word_rows[:, HEAD:])
        nc.sync.dma_start(out=w8_raw[:], in_=w8.rearrange("(p j) n -> p j n", j=PACK))
        nc.sync.dma_start(out=w4_codes[:].bitcast(I32), in_=w4_words[0].bitcast(I32))

        for h in range(2):
            offsets = lists[:, h * HALF // LIST_ROWS : (h + 1) * HALF // LIST_ROWS]
            nc.vector.tensor_copy(out=picked_scales[h][:].rearrange("p (g j m) -> p g m j", j=PAIR, m=P), in_=tab_scales[:].bitcast(U8).indirect(offsets))
        for h in range(2):
            for q in range(QUADRANTS):
                nc.sync.dma_start(
                    out=token_planes[h][32 * q : 32 * q + ROWS, :],
                    in_=picked_scales[h][:].bitcast(I32)[STAGED + ROWS * q : STAGED + ROWS * (q + 1), :],
                )
        nc.sync.dma_start(out=res_first[:].rearrange("p (g b) n -> p g b n", b=PAIR), in_=r[:HALF, :].rearrange("(g p b) n -> p g b n", p=P, b=PAIR))
        nc.sync.dma_start(out=res_rest[:].rearrange("p (g b) n -> p g b n", b=PAIR), in_=r[HALF:, :].rearrange("(g p b) n -> p g b n", p=P, b=PAIR))

        nc.scalar.copy(
            out=w8_grouped[:, :SHARE, :].rearrange("p (c i) j -> p c j i", i=4),
            in_=w8_raw[:, :, :SHARE].rearrange("p j (c i) -> p c j i", i=4),
        )
        nc.gpsimd.tensor_scalar(
            w8_grouped[:, SHARE:, :].rearrange("p (c i) j -> p c j i", i=4),
            w8_raw[:, :, SHARE:].rearrange("p j (c i) -> p c j i", i=4),
            1.0,
            0.0,
            MULT,
            ADD,
        )

        def gather(i):
            width = PAIR * P // LIST_ROWS
            offsets = lists[:, i * width : (i + 1) * width]
            nc.vector.tensor_copy(out=picked_words[i][:].rearrange("p (j m) -> p m j", j=PAIR), in_=tab_words[:].bitcast(U32).indirect(offsets))

        def psum_of(at, b, n):
            bank, place = at[b]
            return banks[bank][:, place : place + n, :]

        def part(tiles, b, n):
            return tiles[b // PAIR][:, b % PAIR : b % PAIR + n, :]

        def multiply(at, b, weights, weight_scales):
            half, column = divmod(b * P, HALF)
            nc.tensor.matmul_mx(
                out=psum_of(at, b, 1)[:, 0, :],
                lhsT=picked_words[b // PAIR][:, b % PAIR * P : (b % PAIR + 1) * P].bitcast(E4M3_X4),
                lhsT_scale=token_planes[half][:].bitcast(U8)[:, column : column + P],
                rhs=weights,
                rhs_scale=weight_scales,
                start=True,
                stop=True,
            )

        def gate(b, n):
            for j in range(n):
                multiply(e_at, b + j, w4_codes[:].bitcast(E2M1_X4), w4_plane[:].bitcast(U8))
            nc.scalar.activation(part(gates, b, n), psum_of(e_at, b, n), SILU)

        def up(b, n):
            for j in range(n):
                multiply(u_at, b + j, w8_codes[:].bitcast(E4M3_X4), w8_plane[:])

        def product(b, n):
            nc.vector.tensor_tensor(part(prods, b, n), part(gates, b, n), psum_of(u_at, b, n), MULT)

        def add(adder, b, n):
            adder.tensor_tensor(part(sums, b, n), part(prods, b, n), part(res, b, n), ADD)

        def store(i):
            rows = out[PAIR * i * P : PAIR * (i + 1) * P, :]
            nc.sync.dma_start(out=rows.rearrange("(p b) n -> p b n", p=P), in_=sums[i][:])

        for i in range(PAIRS):
            if i == 2:
                nc.vector.quantize_mx(
                    out=w8_codes[:].bitcast(E4M3_X4),
                    scales=w8_plane[:],
                    in_=w8_grouped[:].rearrange("p n j -> p (n j)"),
                )
            gather(i)

        gate(0, 2)
        gate(2, 2)
        up(0, 2)
        up(2, 2)
        product(0, 2)
        product(2, 2)
        add(nc.vector, 0, 2)
        store(0)
        add(nc.vector, 2, 1)
        add(nc.gpsimd, 3, 1)
        store(1)

        gate(4, 1)
        gate(5, 1)
        up(4, 1)
        gate(6, 1)
        up(5, 1)
        gate(7, 1)
        up(6, 1)
        up(7, 1)
        product(4, 2)
        product(6, 1)
        product(7, 1)
        add(nc.vector, 4, 2)
        store(2)
        add(nc.vector, 6, 2)
        store(3)
